import numpy as np
import ml_dtypes


def mxq(x, axis, fmt="e4m3"):
    dtype, down = {"e4m3": (ml_dtypes.float8_e4m3fn, 7), "e5m2": (ml_dtypes.float8_e5m2, 14)}[fmt]
    v = np.moveaxis(np.asarray(x, np.float32).astype(ml_dtypes.bfloat16).astype(np.float64), axis, -1)
    blocks = v.reshape(v.shape[:-1] + (-1, 32))
    amax = np.abs(blocks).max(-1, keepdims=True)
    byte = np.maximum(np.where(amax > 0, np.frexp(amax)[1] - 1 + 127, 0) - down, 1)
    scale = np.exp2(byte - 127.0)
    codes = (blocks / scale).astype(np.float32).astype(dtype).astype(np.float64)
    return np.moveaxis((codes * scale).reshape(v.shape), -1, axis)


WIDE = False


def mx_kscale(k):
    if not WIDE:
        return np.ones(k)
    levels = np.array([10, -10, 5, -5, 0])
    if k % 512:
        return np.exp2(np.random.permutation(np.resize(levels, k // 32))).repeat(32)
    a = np.empty((k // 512, 16))
    for p in range(k // 512):
        a[p, :8] = np.random.permutation(np.resize(levels, 8))
        for g in range(8):
            far = levels[np.abs(levels - a[p, g]) >= 10]
            a[p, g + 8] = far[np.random.randint(len(far))]
    return np.exp2(a.ravel()).repeat(32)


BF16 = ml_dtypes.bfloat16


def bf(x):
    return np.asarray(x, np.float32).astype(BF16)


def f64(x):
    return np.asarray(x).astype(np.float64)


E2M1 = np.array([0.0, 0.5, 1.0, 1.5, 2.0, 3.0, 4.0, 6.0, -0.0, -0.5, -1.0, -1.5, -2.0, -3.0, -4.0, -6.0])


def pack_weight(w, fmt):
    k, n = w.shape
    w = f64(bf(w)).reshape(k // 32, 32, n)
    amax = np.abs(w).max(1)
    if fmt == "e4m3":
        byte = np.frexp(amax)[1] - 1 + 127 - 7
    else:
        mant, ex = np.frexp(amax / 6.0)
        byte = np.where(mant > 0.5, ex, ex - 1) + 127
    byte = np.clip(np.where(amax > 0, byte, 1), 1, 254)
    scaled = (w * np.exp2(127.0 - byte)[:, None, :]).reshape(k, n).astype(np.float32)
    by_word = np.ascontiguousarray(scaled.reshape(k // 512, 128, 4, n).transpose(0, 1, 3, 2))
    if fmt == "e4m3":
        words = by_word.astype(ml_dtypes.float8_e4m3fn).view(np.uint8)
    else:
        c = by_word.astype(ml_dtypes.float4_e2m1fn).view(np.uint8) & 0xF
        words = c[..., 0::2] | (c[..., 1::2] << 4)
    return np.ascontiguousarray(words), np.ascontiguousarray(byte.astype(np.uint8).reshape(k // 512, 16, n))


def unpack_weight(words, scales, fmt):
    g, p, n, _ = words.shape
    if fmt == "e4m3":
        vals = np.ascontiguousarray(words).view(ml_dtypes.float8_e4m3fn).astype(np.float64)
    else:
        nib = np.empty((g, p, n, 4), np.uint8)
        nib[..., 0::2] = words & 0xF
        nib[..., 1::2] = words >> 4
        vals = E2M1[nib]
    vals = vals * np.repeat(np.exp2(scales.astype(np.float64) - 127.0), 8, axis=1)[..., None]
    return vals.transpose(0, 1, 3, 2).reshape(g * 512, n)
def pack4(w):
    words, scales = pack_weight(w, "e2m1")
    return words.reshape(words.shape[0], 128, -1), scales


def unpack4(words, scales):
    return unpack_weight(words.reshape(words.shape[0], 128, -1, 2), scales, "e2m1")


def planes(Y):
    n, m = Y.shape
    b = f64(bf(Y)).reshape(n // 32, 32, m)
    amax = np.abs(b).max(1)
    byte = np.clip(np.where(amax > 0, np.frexp(amax)[1] - 1 + 127 - 7, 1), 1, 254)
    codes = (b * np.exp2(127.0 - byte)[:, None, :]).reshape(n, m).astype(np.float32).astype(ml_dtypes.float8_e4m3fn).view(np.uint8)
    words = codes.reshape(n // 512, 128, 4, m).transpose(0, 1, 3, 2)
    return np.ascontiguousarray(words), np.ascontiguousarray(byte.astype(np.uint8).reshape(n // 512, 16, m))


M, K, F, N = 1280, 1536, 1024, 2048
SLOPE = 0.125


def setup_inputs():
    s = mx_kscale(K)
    t = mx_kscale(F)
    spectra = np.random.randn(M, K) * s
    w1 = np.random.randn(K, F) / np.sqrt(K) / s[:, None] * t[None, :]
    b1 = 0.3 * np.random.randn(F) * t
    w2 = 0.7 * np.random.randn(F, N) / np.sqrt(F) / t[:, None]
    w1_words, w1_scales = pack4(w1)
    w2_words, w2_scales = pack4(w2)
    base_rate = np.exp(0.8 * np.random.randn(N))
    throughput = np.exp(0.3 * np.random.randn(M))
    return {"spectra": bf(spectra), "w1_words": w1_words, "w1_scales": w1_scales, "b1": bf(b1),
            "w2_words": w2_words, "w2_scales": w2_scales,
            "base_rate": bf(base_rate), "throughput": bf(throughput)}


def reference(spectra, w1_words, w1_scales, b1, w2_words, w2_scales, base_rate, throughput):
    H = (mxq(f64(spectra), 1, "e4m3") @ unpack4(w1_words, w1_scales)) + f64(b1)
    A = np.maximum(H, SLOPE * H)
    Z = mxq(A, 1, "e4m3") @ unpack4(w2_words, w2_scales)
    y = np.exp(Z) * f64(base_rate) * f64(throughput)[:, None]
    Y = y.T
    words, scales = planes(Y)
    return y, words, scales

@@ -1,0 +1,458 @@
+from contextlib import ExitStack
+
+import concourse.mybir as mybir
+from concourse.masks import make_identity
+
+M, K, F, N = 1280, 1536, 1024, 2048
+SLOPE = 0.125
+FLOPS = 2 * M * K * F + 2 * M * F * N
+
+F32 = mybir.dt.float32
+BF16 = mybir.dt.bfloat16
+I32 = mybir.dt.int32
+U32 = mybir.dt.uint32
+U8 = mybir.dt.uint8
+FP8X4 = mybir.dt.float8_e4m3fn_x4
+FP4X4 = mybir.dt.float4_e2m1fn_x4
+ACT = mybir.ActivationFunctionType
+ALU = mybir.AluOpType
+
+P = 128
+PACK = 4
+PASS = P * PACK
+BANK = 512
+KG, FG, NG = K // PASS, F // PASS, N // PASS
+TILES = M // P
+PAIR = 2 * P
+PAIRS = M // PAIR
+ROTATING_BANKS = 6
+THR_ROW = 32
+CASTS = "VVVS"
+CY = "SS"
+
+
+def CAST(i, n):
+    return CASTS[n] if i < TILES - 1 else "VVVV"[n]
+
+
+def tile_impedance_ageing_rates_h1_kernel(
+    tc, spectra, w1_words, w1_scales, b1, w2_words, w2_scales, base_rate, throughput, out_0, out_1, out_2
+):
+    nc = tc.nc
+    with ExitStack() as ctx:
+        keep = ctx.enter_context(tc.tile_pool(name="keep", bufs=1))
+        work = ctx.enter_context(tc.tile_pool(name="work", bufs=3))
+        psum = ctx.enter_context(tc.psum_pool(name="psum", bufs=1))
+        ctx.enter_context(tc.manual_schedule(engines={mybir.EngineType.PE, mybir.EngineType.SP}))
+
+        x_raw = keep.tile([P, TILES, K], BF16, name="x_raw", align_bytes=64)
+        w1_raw = keep.tile([P, FG, KG, 2 * PASS], U8, name="w1_raw", align_bytes=64)
+        w1s_raw = keep.tile([P, KG, F], U8, name="w1s_raw", align_bytes=64)
+        w1_codes = keep.tile([P, FG, KG, PACK, 2 * P], U8, name="w1_codes", align_bytes=64)
+        w1_plane = keep.tile([P, FG, PACK, KG, P], U8, name="w1_plane", align_bytes=64)
+        w2_codes = keep.tile([P, FG, 2 * N], U8, name="w2_codes", align_bytes=64)
+        w2_plane = keep.tile([P, FG, N], U8, name="w2_plane", align_bytes=64)
+        x_codes = keep.tile([P, KG, M], U32, name="x_codes", align_bytes=64)
+        x_plane = keep.tile([P, KG, M], U8, name="x_plane", align_bytes=64)
+        a_codes = keep.tile([P, FG, M], U32, name="a_codes", align_bytes=64)
+        a_plane = keep.tile([P, FG, M], U8, name="a_plane", align_bytes=64)
+        code_spans = [(0, 2), (2, 4), (4, 6), (6, 8), (8, 9), (9, 10)]
+        plane_spans = [(0, 8), (8, 10)]
+        y_codes = [keep.tile([P, NG, (b - a) * P], U32, name="y_codes%d" % a, align_bytes=64) for a, b in code_spans]
+        y_plane = [keep.tile([P, NG, (b - a) * P], U8, name="y_plane%d" % a, align_bytes=64) for a, b in plane_spans]
+
+        def window(tiles, spans, i, n):
+            j = [a <= i < b for a, b in spans].index(True)
+            lo = (i - spans[j][0]) * P
+            return tiles[j][:, n, lo : lo + P]
+
+        ident_f32 = keep.tile([P, P], F32, name="ident_f32", align_bytes=64)
+        ident_bf16 = keep.tile([P, P], BF16, name="ident_bf16", align_bytes=64)
+        rows = keep.tile([P, P], BF16, name="rows", align_bytes=64)
+        base_cols = keep.tile([P, N // P], BF16, name="base_cols", align_bytes=64)
+        thr = keep.tile([P, TILES], F32, name="thr", align_bytes=64)
+        bias = keep.tile([P, FG, PACK], BF16, name="bias", align_bytes=64)
+        warm = keep.tile([P, 16], F32, name="warm", align_bytes=64)
+        base_wide = [psum.tile([P, 2 * BANK], BF16, name="base_wide%d" % j) for j in range(2)]
+
+        bank_count = [0]
+
+        def next_bank():
+            bank_count[0] += 1
+            return psum.tile([P, BANK], F32, name="bank%d" % (bank_count[0] % ROTATING_BANKS))
+
+        def load_x(i):
+            nc.sync.dma_start(out=x_raw[:, i, :], in_=spectra[i * P : (i + 1) * P, :])
+
+        def load_scales(plane, scales):
+            for q in range(4):
+                nc.sync.dma_start(
+                    out=plane[32 * q : 32 * q + 4, :, :].bitcast(I32),
+                    in_=scales[:, 4 * q : 4 * q + 4, :].rearrange("g r n -> r g n").bitcast(I32),
+                )
+
+        nc.vector.memset(w1s_raw[:].rearrange("p g n -> p (g n)").bitcast(U32), 0)
+        nc.vector.memset(rows[:], 0.0)
+        nc.vector.memset(w2_plane[:].rearrange("p g n -> p (g n)").bitcast(U32), 0)
+        nc.vector.memset(warm[:], 0.0)
+        nc.scalar.activation(out=warm[:, 0:1], in_=warm[:, 8:9], func=ACT.Exp)
+        make_identity(nc, ident_f32[:])
+        make_identity(nc, ident_bf16[:])
+        def load_w1(fg):
+            nc.sync.dma_start(
+                out=w1_raw[:, fg, :, :].bitcast(I32),
+                in_=w1_words[:, :, fg * 2 * PASS : (fg + 1) * 2 * PASS].rearrange("g p n -> p g n").bitcast(I32),
+            )
+
+        load_x(0)
+        load_w1(0)
+        load_scales(w1s_raw, w1_scales)
+        load_x(1)
+        load_w1(1)
+        nc.gpsimd.dma_start(out=bias[:], in_=b1.rearrange("(g p t) -> p g t", g=FG, t=PACK))
+        nc.gpsimd.dma_start(out=rows[0 : N // P, :], in_=base_rate.rearrange("(r c) -> r c", c=P))
+        thr_rows = throughput.rearrange("(r c) -> r c", c=P)
+        nc.gpsimd.dma_start(out=rows[THR_ROW : THR_ROW + 8, :], in_=thr_rows[0:8, :])
+        nc.gpsimd.dma_start(out=rows[THR_ROW + 8 : THR_ROW + TILES, :], in_=thr_rows[8:TILES, :])
+        load_x(2)
+        load_x(3)
+        load_scales(w2_plane, w2_scales)
+        nc.sync.dma_start(out=w2_codes[:].bitcast(I32), in_=w2_words.rearrange("g p n -> p g n").bitcast(I32))
+        for i in range(4, TILES):
+            load_x(i)
+
+        def permute_scales(fg):
+            nc.vector.tensor_copy(
+                out=w1_plane[:, fg],
+                in_=w1s_raw[:, :, fg * PASS : (fg + 1) * PASS].rearrange("p g (m t) -> p t g m", t=PACK),
+            )
+
+        def permute_words(fg):
+            for g in range(KG):
+                nc.vector.tensor_copy(
+                    out=w1_codes[:, fg, g].rearrange("p t (m b) -> p t m b", b=2),
+                    in_=w1_raw[:, fg, g, :].rearrange("p (m t b) -> p t m b", t=PACK, b=2),
+                )
+
+        x_grouped = {}
+
+        def turn_x(units, eng="S"):
+            bank = next_bank()
+            for j, (i, g) in enumerate(units):
+                words = x_raw[:, i, :].bitcast(F32)
+                for u in range(2):
+                    col = (2 * j + u) * P
+                    nc.tensor.transpose(bank[:, col : col + P], words[:, PAIR * g + u : PAIR * (g + 1) : 2], ident_f32[:])
+            xg = work.tile([P, PAIR * PACK], BF16, name="xg", bufs=6, align_bytes=64)
+            count = len(units)
+            dst = xg[:, 0 : count * PASS].bitcast(F32).rearrange("p (j m u) -> p j m u", j=count, u=2)
+            src = bank[:, 0 : count * PAIR].rearrange("p (j u m) -> p j m u", j=count, u=2)
+            if eng == "S":
+                nc.scalar.copy(out=dst, in_=src)
+            else:
+                nc.vector.tensor_copy(out=dst, in_=src)
+            for j, unit in enumerate(units):
+                x_grouped[unit] = (xg, j)
+
+        def quant_x(i, g, count):
+            cols = slice(i * P, (i + count) * P)
+            xg, j = x_grouped[i, g]
+            nc.vector.quantize_mx(
+                out=x_codes[:, g, cols].bitcast(FP8X4), scales=x_plane[:, g, cols], in_=xg[:, j * PASS : (j + count) * PASS]
+            )
+
+        def turn_pair(q, g):
+            turn_x([(2 * q, g), (2 * q + 1, g)])
+
+        def quant_pair(q):
+            for g in range(KG):
+                quant_x(2 * q, g, 2)
+
+        def constants():
+            bank = next_bank()
+            turned = bank[:].bitcast(BF16)[:, 0:P]
+            nc.tensor.transpose(turned, rows[:], ident_bf16[:])
+            nc.vector.tensor_copy(out=base_cols[:], in_=turned[:, 0 : N // P])
+            nc.vector.tensor_copy(out=thr[:], in_=turned[:, THR_ROW : THR_ROW + TILES])
+
+        def spread_base():
+            for c in range(N // P):
+                nc.tensor.transpose(
+                    base_wide[c // 8][:, (c % 8) * P : (c % 8 + 1) * P],
+                    base_cols[:, c : c + 1].to_broadcast([P, P]),
+                    ident_bf16[:],
+                )
+
+        chunk_cells = [(0, P), (P, P), (PAIR, BANK), (PAIR + BANK, BANK)]
+        hidden = {}
+
+        def hidden_matmul(out, fg, t, cols):
+            for g in range(KG):
+                nc.tensor.matmul_mx(
+                    out=out,
+                    lhsT=w1_codes[:, fg, g, t, :].bitcast(FP4X4),
+                    lhsT_scale=w1_plane[:, fg, t, g, :],
+                    rhs=x_codes[:, g, cols].bitcast(FP8X4),
+                    rhs_scale=x_plane[:, g, cols],
+                    start=(g == 0),
+                    stop=(g == KG - 1),
+                )
+
+        def hidden_bank(c, fg, ts):
+            first, width = chunk_cells[c]
+            if ts[0] == 0:
+                hidden[c, fg] = work.tile([P, PACK, BANK], F32, name="h", bufs=3, align_bytes=64)
+            bank = next_bank()
+            step = BANK if width == BANK else P
+            for j, t in enumerate(ts):
+                for lo in range(0, width, step):
+                    hidden_matmul(bank[:, j * width + lo : j * width + lo + step], fg, t, slice(first + lo, first + lo + step))
+            for j, t in enumerate(ts):
+                nc.scalar.activation(
+                    out=hidden[c, fg][:, t, 0:width],
+                    in_=bank[:, j * width : (j + 1) * width],
+                    func=ACT.Identity,
+                    bias=bias[:, fg, t : t + 1],
+                )
+
+        a_grouped = {}
+
+        def leaky(c, fg, half):
+            width = min(PAIR, chunk_cells[c][1])
+            cells = hidden[c, fg][:, :, half * width : (half + 1) * width].rearrange("p t m -> p m t")
+            ag = work.tile([P, PAIR * PACK], BF16, name="ag", bufs=3, align_bytes=64)
+            nc.vector.scalar_tensor_tensor(
+                out=ag[:, 0 : width * PACK].rearrange("p (m t) -> p m t", t=PACK),
+                in0=cells,
+                scalar=SLOPE,
+                in1=cells,
+                op0=ALU.mult,
+                op1=ALU.max,
+            )
+            a_grouped[c, fg, half] = ag
+
+        def quant_a(c, fg, half):
+            width = min(PAIR, chunk_cells[c][1])
+            lo = chunk_cells[c][0] + half * width
+            cols = slice(lo, lo + width)
+            nc.vector.quantize_mx(
+                out=a_codes[:, fg, cols].bitcast(FP8X4), scales=a_plane[:, fg, cols], in_=a_grouped[c, fg, half][:, 0 : width * PACK]
+            )
+
+        growth = {}
+        y_f32 = {}
+        y_bf16 = {}
+        y_grouped = {}
+        y_banks = {}
+
+        def rate_bank(i, n):
+            cells = slice(i * P, (i + 1) * P)
+            bank = next_bank()
+            for fg in range(FG):
+                nc.tensor.matmul_mx(
+                    out=bank[:],
+                    lhsT=a_codes[:, fg, cells].bitcast(FP8X4),
+                    lhsT_scale=a_plane[:, fg, cells],
+                    rhs=w2_codes[:, fg, n * 2 * BANK : (n + 1) * 2 * BANK].bitcast(FP4X4),
+                    rhs_scale=w2_plane[:, fg, n * BANK : (n + 1) * BANK],
+                    start=(fg == 0),
+                    stop=(fg == FG - 1),
+                )
+            e = work.tile([P, BANK], F32, name="e", bufs=8, align_bytes=64)
+            nc.scalar.activation(out=e[:], in_=bank[:], func=ACT.Exp)
+            growth[i, n] = e
+
+        def scale_y(i, n):
+            if n == 0:
+                y_f32[i] = work.tile([P, N], F32, name="y", bufs=3, align_bytes=64)
+                y_bf16[i] = work.tile([P, N], BF16, name="yb", bufs=3, align_bytes=64)
+            nc.vector.scalar_tensor_tensor(
+                out=y_f32[i][:, n * BANK : (n + 1) * BANK],
+                in0=growth[i, n][:],
+                scalar=thr[:, i : i + 1],
+                in1=base_wide[n // 2][:, (n % 2) * BANK : (n % 2 + 1) * BANK],
+                op0=ALU.mult,
+                op1=ALU.mult,
+            )
+
+        def round_y(i, n):
+            cols = slice(n * BANK, (n + 1) * BANK)
+            dst = y_bf16[i][:, cols].rearrange("p (u m e) -> p u m e", u=2, e=2)
+            src = y_f32[i][:, cols].rearrange("p (m u e) -> p u m e", u=2, e=2)
+            if CAST(i, n) == "V":
+                nc.vector.tensor_copy(out=dst, in_=src)
+            elif CAST(i, n) == "S":
+                nc.scalar.copy(out=dst, in_=src)
+            else:
+                nc.gpsimd.tensor_scalar(out=dst, in0=src, scalar1=1.0, scalar2=0.0, op0=ALU.mult, op1=ALU.add)
+
+        def store_y(i, lo, hi):
+            nc.sync.dma_start(out=out_0[i * P : (i + 1) * P, lo:hi], in_=y_f32[i][:, lo:hi])
+
+        def turn_y(i, half):
+            if half == 0:
+                y_grouped[i] = work.tile([P, N], BF16, name="yg", bufs=3, align_bytes=64)
+            bank = next_bank()
+            words = y_bf16[i][:].bitcast(F32)
+            for j in range(4):
+                nc.tensor.transpose(bank[:, j * P : (j + 1) * P], words[:, half * BANK + j * P : half * BANK + (j + 1) * P], ident_f32[:])
+            y_banks[i, half] = bank
+            if CY[half] == "S":
+                drain_y(i, half)
+
+        def drain_y(i, half):
+            dst = y_grouped[i][:].bitcast(F32)[:, half * BANK : (half + 1) * BANK].rearrange("p (g m u) -> p g m u", g=2, u=2)
+            src = y_banks[i, half][:].rearrange("p (g u m) -> p g m u", g=2, u=2)
+            if CY[half] == "S":
+                nc.scalar.copy(out=dst, in_=src)
+            else:
+                nc.vector.tensor_copy(out=dst, in_=src)
+
+        def quant_y(i, n):
+            nc.vector.quantize_mx(
+                out=window(y_codes, code_spans, i, n).bitcast(FP8X4),
+                scales=window(y_plane, plane_spans, i, n),
+                in_=y_grouped[i][:, n * BANK : (n + 1) * BANK],
+            )
+
+        def store_codes(j):
+            lo, hi = code_spans[j][0] * P, code_spans[j][1] * P
+            nc.sync.dma_start(
+                out=out_1.rearrange("g p m t -> p g (m t)")[:, :, PACK * lo : PACK * hi].bitcast(I32),
+                in_=y_codes[j][:].bitcast(I32),
+            )
+
+        def store_scales(j):
+            lo, hi = plane_spans[j][0] * P, plane_spans[j][1] * P
+            for q in range(4):
+                nc.sync.dma_start(
+                    out=out_2[:, 4 * q : 4 * q + 4, lo:hi].rearrange("g r m -> r g m").bitcast(I32),
+                    in_=y_plane[j][32 * q : 32 * q + 4, :, :].bitcast(I32),
+                )
+
+        ALL = (0, 1, 2, 3)
+        def rates(i):
+            for n in range(NG):
+                rate_bank(i, n)
+
+        def scales(i):
+            last = i == TILES - 1
+            for n in range(NG):
+                if (i, n) != (2, 0):
+                    scale_y(i, n)
+                if last:
+                    store_y(i, n * BANK, (n + 1) * BANK)
+                if n > 0:
+                    round_y(i, n - 1)
+                if last and n == 2:
+                    turn_y(i, 0)
+            if not last:
+                store_y(i, 0, N)
+
+        def planes(i):
+            for n in range(NG):
+                quant_y(i, n)
+            for j, span in enumerate(code_spans):
+                if span[1] == i + 1:
+                    store_codes(j)
+            for j, span in enumerate(plane_spans):
+                if span[1] == i + 1:
+                    store_scales(j)
+
+
+        turn_x([(0, 0), (0, 1)])
+        turn_x([(0, 2)])
+        permute_words(0)
+        for g in range(KG):
+            quant_x(0, g, 1)
+        permute_scales(0)
+        turn_x([(1, 0), (1, 1)])
+        turn_x([(1, 2)])
+        constants()
+        hidden_bank(0, 0, ALL)
+        permute_scales(1)
+        permute_words(1)
+        for g in range(KG):
+            quant_x(1, g, 1)
+        hidden_bank(1, 0, ALL)
+        spread_base()
+        hidden_bank(0, 1, ALL)
+        hidden_bank(1, 1, ALL)
+        for g in range(KG):
+            turn_pair(1, g)
+        leaky(0, 0, 0)
+        leaky(1, 0, 0)
+        quant_a(0, 0, 0)
+        leaky(0, 1, 0)
+        quant_a(1, 0, 0)
+        leaky(1, 1, 0)
+        quant_a(0, 1, 0)
+        rates(0)
+        for g in range(KG):
+            turn_pair(2, g)
+        quant_x(2, 0, 2)
+        quant_a(1, 1, 0)
+        rates(1)
+        quant_x(2, 1, 2)
+        quant_x(2, 2, 2)
+        scale_y(0, 0)
+        scale_y(0, 1)
+        round_y(0, 0)
+        quant_x(4, 0, 2)
+        scale_y(0, 2)
+        quant_x(4, 1, 2)
+        round_y(0, 1)
+        quant_x(4, 2, 2)
+        for fg in range(FG):
+            for t in ALL:
+                hidden_bank(2, fg, (t,))
+        scale_y(0, 3)
+        round_y(0, 2)
+        store_y(0, 0, N)
+        scales(1)
+        round_y(0, 3)
+        leaky(2, 0, 0)
+        round_y(1, 3)
+        for g in range(KG):
+            turn_pair(3, g)
+        turn_y(0, 0)
+        turn_y(0, 1)
+        leaky(2, 0, 1)
+        quant_a(2, 0, 0)
+        leaky(2, 1, 0)
+        quant_a(2, 0, 1)
+        quant_x(6, 0, 2)
+        quant_a(2, 1, 0)
+        rates(2)
+        leaky(2, 1, 1)
+        for g in range(KG):
+            turn_pair(4, g)
+        quant_x(6, 1, 2)
+        quant_x(6, 2, 2)
+        planes(0)
+        quant_a(2, 1, 1)
+        banks = {2: [(0, 0), (0, 1), (0, 2), (0, 3)], 3: [(1, 0), (1, 1), (1, 2), (1, 3)]}
+        acts = {3: [(3, 0, 0)], 4: [(3, 1, 0)], 5: [(3, 0, 1)], 6: [(3, 1, 1)]}
+        for i in range(2, TILES):
+            if i > 2:
+                round_y(i - 1, NG - 1)
+            if i + 1 < TILES:
+                rates(i + 1)
+            if i == 2:
+                scale_y(2, 0)
+                quant_pair(4)
+            for fg, t in banks.get(i, []):
+                hidden_bank(3, fg, (t,))
+            turn_y(i - 1, 0)
+            turn_y(i - 1, 1)
+            for act in acts.get(i, []):
+                leaky(*act)
+            scales(i)
+            for act in acts.get(i, []):
+                quant_a(*act)
+            if i > 2:
+                planes(i - 2)
+        round_y(TILES - 1, NG - 1)
+        planes(TILES - 2)
+        turn_y(TILES - 1, 1)
+        planes(TILES - 1)

@@ -21,18 +21,13 @@ P = 128
 PACK = 4
 PASS = P * PACK
 BANK = 512
+HALF = N // 2
 KG, FG, NG = K // PASS, F // PASS, N // PASS
 TILES = M // P
-PAIR = 2 * P
-PAIRS = M // PAIR
 ROTATING_BANKS = 6
 THR_ROW = 32
-CASTS = "VVVS"
-CY = "SS"
-
-
-def CAST(i, n):
-    return CASTS[n] if i < TILES - 1 else "VVVV"[n]
+CASTS = ["SV"] * 10
+CY = ["SS"] * 10
 
 
 def tile_impedance_ageing_rates_h1_kernel(
@@ -43,37 +38,32 @@ def tile_impedance_ageing_rates_h1_kernel(
         keep = ctx.enter_context(tc.tile_pool(name="keep", bufs=1))
         work = ctx.enter_context(tc.tile_pool(name="work", bufs=3))
         psum = ctx.enter_context(tc.psum_pool(name="psum", bufs=1))
-        ctx.enter_context(tc.manual_schedule(engines={mybir.EngineType.PE, mybir.EngineType.SP}))
+        ctx.enter_context(tc.manual_schedule())
 
         x_raw = keep.tile([P, TILES, K], BF16, name="x_raw", align_bytes=64)
-        w1_raw = keep.tile([P, FG, KG, 2 * PASS], U8, name="w1_raw", align_bytes=64)
-        w1s_raw = keep.tile([P, KG, F], U8, name="w1s_raw", align_bytes=64)
-        w1_codes = keep.tile([P, FG, KG, PACK, 2 * P], U8, name="w1_codes", align_bytes=64)
-        w1_plane = keep.tile([P, FG, PACK, KG, P], U8, name="w1_plane", align_bytes=64)
+        w1_codes = keep.tile([P, KG, 2 * F], U8, name="w1_codes", align_bytes=64)
+        w1_plane = keep.tile([P, KG, F], U8, name="w1_plane", align_bytes=64)
         w2_codes = keep.tile([P, FG, 2 * N], U8, name="w2_codes", align_bytes=64)
         w2_plane = keep.tile([P, FG, N], U8, name="w2_plane", align_bytes=64)
-        x_codes = keep.tile([P, KG, M], U32, name="x_codes", align_bytes=64)
-        x_plane = keep.tile([P, KG, M], U8, name="x_plane", align_bytes=64)
-        a_codes = keep.tile([P, FG, M], U32, name="a_codes", align_bytes=64)
-        a_plane = keep.tile([P, FG, M], U8, name="a_plane", align_bytes=64)
-        code_spans = [(0, 2), (2, 4), (4, 6), (6, 8), (8, 9), (9, 10)]
-        plane_spans = [(0, 8), (8, 10)]
+        code_spans = [(0, 2), (2, 4), (4, 6), (6, 7), (7, 8), (8, 9), (9, 10)]
+        plane_spans = [(0, 7), (7, 10)]
         y_codes = [keep.tile([P, NG, (b - a) * P], U32, name="y_codes%d" % a, align_bytes=64) for a, b in code_spans]
         y_plane = [keep.tile([P, NG, (b - a) * P], U8, name="y_plane%d" % a, align_bytes=64) for a, b in plane_spans]
+        ident_f32 = keep.tile([P, P], F32, name="ident_f32", align_bytes=64)
+        ident_bf16 = keep.tile([P, P], BF16, name="ident_bf16", align_bytes=64)
+        bias_rows = keep.tile([P, P], BF16, name="bias_rows", align_bytes=64)
+        bias_cols = keep.tile([P, F // P], BF16, name="bias_cols", align_bytes=64)
+        rows = keep.tile([P, P], BF16, name="rows", align_bytes=64)
+        base_cols = keep.tile([P, N // P], BF16, name="base_cols", align_bytes=64)
+        thr = keep.tile([P, TILES], F32, name="thr", align_bytes=64)
+        bias_wide = keep.tile([P, F], BF16, name="bias_wide", align_bytes=64)
+        warm = keep.tile([P, 16], F32, name="warm", align_bytes=64)
+        base_wide = [psum.tile([P, HALF], BF16, name="base_wide%d" % j) for j in range(2)]
 
         def window(tiles, spans, i, n):
             j = [a <= i < b for a, b in spans].index(True)
             lo = (i - spans[j][0]) * P
             return tiles[j][:, n, lo : lo + P]
-
-        ident_f32 = keep.tile([P, P], F32, name="ident_f32", align_bytes=64)
-        ident_bf16 = keep.tile([P, P], BF16, name="ident_bf16", align_bytes=64)
-        rows = keep.tile([P, P], BF16, name="rows", align_bytes=64)
-        base_cols = keep.tile([P, N // P], BF16, name="base_cols", align_bytes=64)
-        thr = keep.tile([P, TILES], F32, name="thr", align_bytes=64)
-        bias = keep.tile([P, FG, PACK], BF16, name="bias", align_bytes=64)
-        warm = keep.tile([P, 16], F32, name="warm", align_bytes=64)
-        base_wide = [psum.tile([P, 2 * BANK], BF16, name="base_wide%d" % j) for j in range(2)]
 
         bank_count = [0]
 
@@ -91,29 +81,21 @@ def tile_impedance_ageing_rates_h1_kernel(
                     in_=scales[:, 4 * q : 4 * q + 4, :].rearrange("g r n -> r g n").bitcast(I32),
                 )
 
-        nc.vector.memset(w1s_raw[:].rearrange("p g n -> p (g n)").bitcast(U32), 0)
+        nc.vector.memset(w1_plane[:].rearrange("p g n -> p (g n)").bitcast(U32), 0)
+        nc.vector.memset(bias_rows[:], 0.0)
+        nc.vector.memset(warm[:], 0.0)
         nc.vector.memset(rows[:], 0.0)
         nc.vector.memset(w2_plane[:].rearrange("p g n -> p (g n)").bitcast(U32), 0)
-        nc.vector.memset(warm[:], 0.0)
-        nc.scalar.activation(out=warm[:, 0:1], in_=warm[:, 8:9], func=ACT.Exp)
         make_identity(nc, ident_f32[:])
         make_identity(nc, ident_bf16[:])
-        def load_w1(fg):
-            nc.sync.dma_start(
-                out=w1_raw[:, fg, :, :].bitcast(I32),
-                in_=w1_words[:, :, fg * 2 * PASS : (fg + 1) * 2 * PASS].rearrange("g p n -> p g n").bitcast(I32),
-            )
-
         load_x(0)
-        load_w1(0)
-        load_scales(w1s_raw, w1_scales)
+        nc.scalar.dma_start(out=bias_rows[0 : F // P, :], in_=b1.rearrange("(r c) -> r c", c=P))
+        nc.scalar.activation(out=warm[:, 0:1], in_=warm[:, 8:9], func=ACT.Exp)
+        load_scales(w1_plane, w1_scales)
         load_x(1)
-        load_w1(1)
-        nc.gpsimd.dma_start(out=bias[:], in_=b1.rearrange("(g p t) -> p g t", g=FG, t=PACK))
+        nc.sync.dma_start(out=w1_codes[:].bitcast(I32), in_=w1_words.rearrange("g p n -> p g n").bitcast(I32))
         nc.gpsimd.dma_start(out=rows[0 : N // P, :], in_=base_rate.rearrange("(r c) -> r c", c=P))
-        thr_rows = throughput.rearrange("(r c) -> r c", c=P)
-        nc.gpsimd.dma_start(out=rows[THR_ROW : THR_ROW + 8, :], in_=thr_rows[0:8, :])
-        nc.gpsimd.dma_start(out=rows[THR_ROW + 8 : THR_ROW + TILES, :], in_=thr_rows[8:TILES, :])
+        nc.gpsimd.dma_start(out=rows[THR_ROW : THR_ROW + TILES, :], in_=throughput.rearrange("(r c) -> r c", c=P))
         load_x(2)
         load_x(3)
         load_scales(w2_plane, w2_scales)
@@ -121,170 +103,155 @@ def tile_impedance_ageing_rates_h1_kernel(
         for i in range(4, TILES):
             load_x(i)
 
-        def permute_scales(fg):
-            nc.vector.tensor_copy(
-                out=w1_plane[:, fg],
-                in_=w1s_raw[:, :, fg * PASS : (fg + 1) * PASS].rearrange("p g (m t) -> p t g m", t=PACK),
-            )
+        def turn_bias():
+            turned = next_bank()[:].bitcast(BF16)[:, 0:P]
+            nc.tensor.transpose(turned, bias_rows[:], ident_bf16[:])
+            nc.vector.tensor_copy(out=bias_cols[:], in_=turned[:, 0 : F // P])
 
-        def permute_words(fg):
-            for g in range(KG):
-                nc.vector.tensor_copy(
-                    out=w1_codes[:, fg, g].rearrange("p t (m b) -> p t m b", b=2),
-                    in_=w1_raw[:, fg, g, :].rearrange("p (m t b) -> p t m b", t=PACK, b=2),
-                )
-
-        x_grouped = {}
-
-        def turn_x(units, eng="S"):
-            bank = next_bank()
-            for j, (i, g) in enumerate(units):
-                words = x_raw[:, i, :].bitcast(F32)
-                for u in range(2):
-                    col = (2 * j + u) * P
-                    nc.tensor.transpose(bank[:, col : col + P], words[:, PAIR * g + u : PAIR * (g + 1) : 2], ident_f32[:])
-            xg = work.tile([P, PAIR * PACK], BF16, name="xg", bufs=6, align_bytes=64)
-            count = len(units)
-            dst = xg[:, 0 : count * PASS].bitcast(F32).rearrange("p (j m u) -> p j m u", j=count, u=2)
-            src = bank[:, 0 : count * PAIR].rearrange("p (j u m) -> p j m u", j=count, u=2)
-            if eng == "S":
-                nc.scalar.copy(out=dst, in_=src)
-            else:
-                nc.vector.tensor_copy(out=dst, in_=src)
-            for j, unit in enumerate(units):
-                x_grouped[unit] = (xg, j)
-
-        def quant_x(i, g, count):
-            cols = slice(i * P, (i + count) * P)
-            xg, j = x_grouped[i, g]
-            nc.vector.quantize_mx(
-                out=x_codes[:, g, cols].bitcast(FP8X4), scales=x_plane[:, g, cols], in_=xg[:, j * PASS : (j + count) * PASS]
-            )
-
-        def turn_pair(q, g):
-            turn_x([(2 * q, g), (2 * q + 1, g)])
-
-        def quant_pair(q):
-            for g in range(KG):
-                quant_x(2 * q, g, 2)
-
-        def constants():
-            bank = next_bank()
-            turned = bank[:].bitcast(BF16)[:, 0:P]
+        def turn_rows():
+            turned = next_bank()[:].bitcast(BF16)[:, 0:P]
             nc.tensor.transpose(turned, rows[:], ident_bf16[:])
             nc.vector.tensor_copy(out=base_cols[:], in_=turned[:, 0 : N // P])
             nc.vector.tensor_copy(out=thr[:], in_=turned[:, THR_ROW : THR_ROW + TILES])
 
-        def spread_base():
-            for c in range(N // P):
-                nc.tensor.transpose(
-                    base_wide[c // 8][:, (c % 8) * P : (c % 8 + 1) * P],
-                    base_cols[:, c : c + 1].to_broadcast([P, P]),
-                    ident_bf16[:],
-                )
+        def spread(wide, cols, first):
+            for c in range(HALF // P):
+                nc.tensor.transpose(wide[:, c * P : (c + 1) * P], cols[:, first + c : first + c + 1].to_broadcast([P, P]), ident_bf16[:])
 
-        chunk_cells = [(0, P), (P, P), (PAIR, BANK), (PAIR + BANK, BANK)]
-        hidden = {}
-
-        def hidden_matmul(out, fg, t, cols):
-            for g in range(KG):
-                nc.tensor.matmul_mx(
-                    out=out,
-                    lhsT=w1_codes[:, fg, g, t, :].bitcast(FP4X4),
-                    lhsT_scale=w1_plane[:, fg, t, g, :],
-                    rhs=x_codes[:, g, cols].bitcast(FP8X4),
-                    rhs_scale=x_plane[:, g, cols],
-                    start=(g == 0),
-                    stop=(g == KG - 1),
-                )
-
-        def hidden_bank(c, fg, ts):
-            first, width = chunk_cells[c]
-            if ts[0] == 0:
-                hidden[c, fg] = work.tile([P, PACK, BANK], F32, name="h", bufs=3, align_bytes=64)
-            bank = next_bank()
-            step = BANK if width == BANK else P
-            for j, t in enumerate(ts):
-                for lo in range(0, width, step):
-                    hidden_matmul(bank[:, j * width + lo : j * width + lo + step], fg, t, slice(first + lo, first + lo + step))
-            for j, t in enumerate(ts):
-                nc.scalar.activation(
-                    out=hidden[c, fg][:, t, 0:width],
-                    in_=bank[:, j * width : (j + 1) * width],
-                    func=ACT.Identity,
-                    bias=bias[:, fg, t : t + 1],
-                )
-
-        a_grouped = {}
-
-        def leaky(c, fg, half):
-            width = min(PAIR, chunk_cells[c][1])
-            cells = hidden[c, fg][:, :, half * width : (half + 1) * width].rearrange("p t m -> p m t")
-            ag = work.tile([P, PAIR * PACK], BF16, name="ag", bufs=3, align_bytes=64)
-            nc.vector.scalar_tensor_tensor(
-                out=ag[:, 0 : width * PACK].rearrange("p (m t) -> p m t", t=PACK),
-                in0=cells,
-                scalar=SLOPE,
-                in1=cells,
-                op0=ALU.mult,
-                op1=ALU.max,
-            )
-            a_grouped[c, fg, half] = ag
-
-        def quant_a(c, fg, half):
-            width = min(PAIR, chunk_cells[c][1])
-            lo = chunk_cells[c][0] + half * width
-            cols = slice(lo, lo + width)
-            nc.vector.quantize_mx(
-                out=a_codes[:, fg, cols].bitcast(FP8X4), scales=a_plane[:, fg, cols], in_=a_grouped[c, fg, half][:, 0 : width * PACK]
-            )
-
-        growth = {}
-        y_f32 = {}
-        y_bf16 = {}
-        y_grouped = {}
-        y_banks = {}
-
-        def rate_bank(i, n):
-            cells = slice(i * P, (i + 1) * P)
-            bank = next_bank()
+        def spread_bias():
+            wide = next_bank()[:].bitcast(BF16)
+            spread(wide, bias_cols, 0)
             for fg in range(FG):
-                nc.tensor.matmul_mx(
-                    out=bank[:],
-                    lhsT=a_codes[:, fg, cells].bitcast(FP8X4),
-                    lhsT_scale=a_plane[:, fg, cells],
-                    rhs=w2_codes[:, fg, n * 2 * BANK : (n + 1) * 2 * BANK].bitcast(FP4X4),
-                    rhs_scale=w2_plane[:, fg, n * BANK : (n + 1) * BANK],
-                    start=(fg == 0),
-                    stop=(fg == FG - 1),
+                nc.vector.tensor_copy(
+                    out=bias_wide[:, fg * BANK : (fg + 1) * BANK].rearrange("p (u m e) -> p u m e", u=2, e=2),
+                    in_=wide[:, fg * BANK : (fg + 1) * BANK].rearrange("p (m u e) -> p u m e", u=2, e=2),
                 )
-            e = work.tile([P, BANK], F32, name="e", bufs=8, align_bytes=64)
-            nc.scalar.activation(out=e[:], in_=bank[:], func=ACT.Exp)
-            growth[i, n] = e
 
-        def scale_y(i, n):
-            if n == 0:
+        def copy_on(engine, out, in_):
+            if engine == "S":
+                nc.scalar.copy(out=out, in_=in_)
+            elif engine == "V":
+                nc.vector.tensor_copy(out=out, in_=in_)
+            else:
+                nc.gpsimd.tensor_scalar(out=out, in0=in_, scalar1=1.0, scalar2=0.0, op0=ALU.mult, op1=ALU.add)
+
+        def interleave(engine, grouped, bank, groups):
+            copy_on(
+                engine,
+                grouped.bitcast(F32).rearrange("p (g m u) -> p g m u", g=groups, u=2),
+                bank[:, 0 : groups * 2 * P].rearrange("p (g u m) -> p g m u", g=groups, u=2),
+            )
+
+        x_grouped, x_mx, h_banks, h_f32, a_bf16, a_grouped, a_mx = {}, {}, {}, {}, {}, {}, {}
+        growth, y_f32, y_bf16, y_banks, y_grouped = {}, {}, {}, {}, {}
+
+        def turn_x(i):
+            words = x_raw[:, i, :].bitcast(F32)
+            x_grouped[i] = work.tile([P, K], BF16, name="xg", bufs=3, align_bytes=64)
+            for first, groups in ((0, 2), (2, 1)):
+                bank = next_bank()
+                for g in range(groups):
+                    for u in range(2):
+                        lo = 2 * P * (first + g)
+                        col = (2 * g + u) * P
+                        nc.tensor.transpose(bank[:, col : col + P], words[:, lo + u : lo + 2 * P : 2], ident_f32[:])
+                interleave("S", x_grouped[i][:, first * PASS : (first + groups) * PASS], bank, groups)
+
+        def quant_x(i):
+            codes = work.tile([P, KG * P], U32, name="xq", bufs=3, align_bytes=64)
+            plane = work.tile([P, KG * P], U8, name="xs", bufs=3, align_bytes=64)
+            for first, groups in ((0, 2), (2, 1)):
+                span = slice(first * P, (first + groups) * P)
+                nc.vector.quantize_mx(
+                    out=codes[:, span].bitcast(FP8X4), scales=plane[:, span], in_=x_grouped[i][:, first * PASS : (first + groups) * PASS]
+                )
+            x_mx[i] = (codes, plane)
+
+        def hidden(i):
+            codes, plane = x_mx[i]
+            for fg in range(FG):
+                bank = next_bank()
+                for g in range(KG):
+                    nc.tensor.matmul_mx(
+                        out=bank[:],
+                        lhsT=codes[:, g * P : (g + 1) * P].bitcast(FP8X4),
+                        lhsT_scale=plane[:, g * P : (g + 1) * P],
+                        rhs=w1_codes[:, g, fg * 2 * BANK : (fg + 1) * 2 * BANK].bitcast(FP4X4),
+                        rhs_scale=w1_plane[:, g, fg * BANK : (fg + 1) * BANK],
+                        start=(g == 0),
+                        stop=(g == KG - 1),
+                    )
+                h_banks[i, fg] = bank
+
+        def add_bias(i, fg):
+            if fg == 0:
+                h_f32[i] = work.tile([P, F], F32, name="h", bufs=2, align_bytes=64)
+            span = slice(fg * BANK, (fg + 1) * BANK)
+            nc.vector.tensor_tensor(
+                out=h_f32[i][:, span].rearrange("p (u m e) -> p u m e", u=2, e=2),
+                in0=h_banks[i, fg][:].rearrange("p (m u e) -> p u m e", u=2, e=2),
+                in1=bias_wide[:, span].rearrange("p (u m e) -> p u m e", u=2, e=2),
+                op=ALU.add,
+            )
+
+        def leaky(i):
+            a_bf16[i] = work.tile([P, F], BF16, name="ab", bufs=2, align_bytes=64)
+            nc.vector.scalar_tensor_tensor(
+                out=a_bf16[i][:], in0=h_f32[i][:], scalar=SLOPE, in1=h_f32[i][:], op0=ALU.mult, op1=ALU.max
+            )
+
+        def turn_a(i):
+            bank = next_bank()
+            words = a_bf16[i][:].bitcast(F32)
+            for j in range(4):
+                nc.tensor.transpose(bank[:, j * P : (j + 1) * P], words[:, j * P : (j + 1) * P], ident_f32[:])
+            a_grouped[i] = work.tile([P, F], BF16, name="ag", bufs=2, align_bytes=64)
+            interleave("S", a_grouped[i][:], bank, FG)
+
+        def quant_a(i):
+            codes = work.tile([P, FG * P], U32, name="aq", bufs=3, align_bytes=64)
+            plane = work.tile([P, FG * P], U8, name="as", bufs=3, align_bytes=64)
+            nc.vector.quantize_mx(out=codes[:].bitcast(FP8X4), scales=plane[:], in_=a_grouped[i][:])
+            a_mx[i] = (codes, plane)
+
+        def rates(i):
+            codes, plane = a_mx[i]
+            for n in range(NG):
+                if n % 2 == 0:
+                    growth[i, n // 2] = work.tile([P, HALF], F32, name="e", bufs=4, align_bytes=64)
+                bank = next_bank()
+                for fg in range(FG):
+                    nc.tensor.matmul_mx(
+                        out=bank[:],
+                        lhsT=codes[:, fg * P : (fg + 1) * P].bitcast(FP8X4),
+                        lhsT_scale=plane[:, fg * P : (fg + 1) * P],
+                        rhs=w2_codes[:, fg, n * 2 * BANK : (n + 1) * 2 * BANK].bitcast(FP4X4),
+                        rhs_scale=w2_plane[:, fg, n * BANK : (n + 1) * BANK],
+                        start=(fg == 0),
+                        stop=(fg == FG - 1),
+                    )
+                nc.scalar.activation(out=growth[i, n // 2][:, (n % 2) * BANK : (n % 2 + 1) * BANK], in_=bank[:], func=ACT.Exp)
+
+        def scale_y(i, half, lo=0, hi=HALF):
+            if half == 0 and lo == 0:
                 y_f32[i] = work.tile([P, N], F32, name="y", bufs=3, align_bytes=64)
                 y_bf16[i] = work.tile([P, N], BF16, name="yb", bufs=3, align_bytes=64)
             nc.vector.scalar_tensor_tensor(
-                out=y_f32[i][:, n * BANK : (n + 1) * BANK],
-                in0=growth[i, n][:],
+                out=y_f32[i][:, half * HALF + lo : half * HALF + hi],
+                in0=growth[i, half][:, lo:hi],
                 scalar=thr[:, i : i + 1],
-                in1=base_wide[n // 2][:, (n % 2) * BANK : (n % 2 + 1) * BANK],
+                in1=base_wide[half][:, lo:hi],
                 op0=ALU.mult,
                 op1=ALU.mult,
             )
 
-        def round_y(i, n):
-            cols = slice(n * BANK, (n + 1) * BANK)
-            dst = y_bf16[i][:, cols].rearrange("p (u m e) -> p u m e", u=2, e=2)
-            src = y_f32[i][:, cols].rearrange("p (m u e) -> p u m e", u=2, e=2)
-            if CAST(i, n) == "V":
-                nc.vector.tensor_copy(out=dst, in_=src)
-            elif CAST(i, n) == "S":
-                nc.scalar.copy(out=dst, in_=src)
-            else:
-                nc.gpsimd.tensor_scalar(out=dst, in0=src, scalar1=1.0, scalar2=0.0, op0=ALU.mult, op1=ALU.add)
+        def round_y(i, half, engine=None, g=None):
+            span = slice(half * HALF, (half + 1) * HALF)
+            dst = y_bf16[i][:, span].rearrange("p (u m e) -> p u m e", u=2, e=2)
+            src = y_f32[i][:, span].rearrange("p (m u e) -> p u m e", u=2, e=2)
+            if g is not None:
+                dst, src = dst[:, :, g * P : (g + 1) * P, :], src[:, :, g * P : (g + 1) * P, :]
+            copy_on(engine or CASTS[i][half], dst, src)
 
         def store_y(i, lo, hi):
             nc.sync.dma_start(out=out_0[i * P : (i + 1) * P, lo:hi], in_=y_f32[i][:, lo:hi])
@@ -294,165 +261,143 @@ def tile_impedance_ageing_rates_h1_kernel(
                 y_grouped[i] = work.tile([P, N], BF16, name="yg", bufs=3, align_bytes=64)
             bank = next_bank()
             words = y_bf16[i][:].bitcast(F32)
-            for j in range(4):
-                nc.tensor.transpose(bank[:, j * P : (j + 1) * P], words[:, half * BANK + j * P : half * BANK + (j + 1) * P], ident_f32[:])
+            for g in range(2):
+                for u in range(2):
+                    lo = half * BANK + (2 * u + g) * P
+                    nc.tensor.transpose(bank[:, (2 * g + u) * P : (2 * g + u + 1) * P], words[:, lo : lo + P], ident_f32[:])
             y_banks[i, half] = bank
-            if CY[half] == "S":
+            if CY[i][half] == "S":
                 drain_y(i, half)
 
         def drain_y(i, half):
-            dst = y_grouped[i][:].bitcast(F32)[:, half * BANK : (half + 1) * BANK].rearrange("p (g m u) -> p g m u", g=2, u=2)
-            src = y_banks[i, half][:].rearrange("p (g u m) -> p g m u", g=2, u=2)
-            if CY[half] == "S":
-                nc.scalar.copy(out=dst, in_=src)
-            else:
-                nc.vector.tensor_copy(out=dst, in_=src)
+            interleave(CY[i][half], y_grouped[i][:, half * HALF : (half + 1) * HALF], y_banks[i, half], 2)
 
-        def quant_y(i, n):
-            nc.vector.quantize_mx(
-                out=window(y_codes, code_spans, i, n).bitcast(FP8X4),
-                scales=window(y_plane, plane_spans, i, n),
-                in_=y_grouped[i][:, n * BANK : (n + 1) * BANK],
-            )
+        def quant_y(i, groups):
+            for n in groups:
+                nc.vector.quantize_mx(
+                    out=window(y_codes, code_spans, i, n).bitcast(FP8X4),
+                    scales=window(y_plane, plane_spans, i, n),
+                    in_=y_grouped[i][:, n * BANK : (n + 1) * BANK],
+                )
 
-        def store_codes(j):
-            lo, hi = code_spans[j][0] * P, code_spans[j][1] * P
+        def store_codes(j, groups):
+            a, b = code_spans[j]
             nc.sync.dma_start(
-                out=out_1.rearrange("g p m t -> p g (m t)")[:, :, PACK * lo : PACK * hi].bitcast(I32),
-                in_=y_codes[j][:].bitcast(I32),
+                out=out_1.rearrange("g p m t -> p g (m t)")[:, groups, PACK * P * a : PACK * P * b].bitcast(I32),
+                in_=y_codes[j][:, groups, :].bitcast(I32),
             )
 
-        def store_scales(j):
-            lo, hi = plane_spans[j][0] * P, plane_spans[j][1] * P
+        def store_scales(j, queue):
+            a, b = plane_spans[j]
             for q in range(4):
-                nc.sync.dma_start(
-                    out=out_2[:, 4 * q : 4 * q + 4, lo:hi].rearrange("g r m -> r g m").bitcast(I32),
+                queue.dma_start(
+                    out=out_2[:, 4 * q : 4 * q + 4, a * P : b * P].rearrange("g r m -> r g m").bitcast(I32),
                     in_=y_plane[j][32 * q : 32 * q + 4, :, :].bitcast(I32),
                 )
 
-        ALL = (0, 1, 2, 3)
-        def rates(i):
-            for n in range(NG):
-                rate_bank(i, n)
-
-        def scales(i):
-            last = i == TILES - 1
-            for n in range(NG):
-                if (i, n) != (2, 0):
-                    scale_y(i, n)
-                if last:
-                    store_y(i, n * BANK, (n + 1) * BANK)
-                if n > 0:
-                    round_y(i, n - 1)
-                if last and n == 2:
-                    turn_y(i, 0)
-            if not last:
-                store_y(i, 0, N)
-
-        def planes(i):
-            for n in range(NG):
-                quant_y(i, n)
+        def store_planes(i):
             for j, span in enumerate(code_spans):
                 if span[1] == i + 1:
-                    store_codes(j)
-            for j, span in enumerate(plane_spans):
-                if span[1] == i + 1:
-                    store_scales(j)
+                    store_codes(j, slice(0, NG))
+            if i + 1 == plane_spans[0][1]:
+                store_scales(0, nc.sync)
 
-
-        turn_x([(0, 0), (0, 1)])
-        turn_x([(0, 2)])
-        permute_words(0)
-        for g in range(KG):
-            quant_x(0, g, 1)
-        permute_scales(0)
-        turn_x([(1, 0), (1, 1)])
-        turn_x([(1, 2)])
-        constants()
-        hidden_bank(0, 0, ALL)
-        permute_scales(1)
-        permute_words(1)
-        for g in range(KG):
-            quant_x(1, g, 1)
-        hidden_bank(1, 0, ALL)
-        spread_base()
-        hidden_bank(0, 1, ALL)
-        hidden_bank(1, 1, ALL)
-        for g in range(KG):
-            turn_pair(1, g)
-        leaky(0, 0, 0)
-        leaky(1, 0, 0)
-        quant_a(0, 0, 0)
-        leaky(0, 1, 0)
-        quant_a(1, 0, 0)
-        leaky(1, 1, 0)
-        quant_a(0, 1, 0)
+        turn_x(0)
+        turn_bias()
+        quant_x(0)
+        spread_bias()
+        hidden(0)
+        turn_x(1)
+        turn_x(2)
+        add_bias(0, 0)
+        add_bias(0, 1)
+        quant_x(1)
+        turn_rows()
+        hidden(1)
+        leaky(0)
+        quant_x(2)
+        add_bias(1, 0)
+        add_bias(1, 1)
+        turn_x(3)
+        turn_a(0)
+        spread(base_wide[0], base_cols, 0)
+        hidden(2)
+        leaky(1)
+        quant_a(0)
+        quant_x(3)
+        turn_a(1)
+        spread(base_wide[1], base_cols, HALF // P)
         rates(0)
-        for g in range(KG):
-            turn_pair(2, g)
-        quant_x(2, 0, 2)
-        quant_a(1, 1, 0)
-        rates(1)
-        quant_x(2, 1, 2)
-        quant_x(2, 2, 2)
-        scale_y(0, 0)
-        scale_y(0, 1)
-        round_y(0, 0)
-        quant_x(4, 0, 2)
-        scale_y(0, 2)
-        quant_x(4, 1, 2)
-        round_y(0, 1)
-        quant_x(4, 2, 2)
-        for fg in range(FG):
-            for t in ALL:
-                hidden_bank(2, fg, (t,))
-        scale_y(0, 3)
-        round_y(0, 2)
-        store_y(0, 0, N)
-        scales(1)
-        round_y(0, 3)
-        leaky(2, 0, 0)
-        round_y(1, 3)
-        for g in range(KG):
-            turn_pair(3, g)
-        turn_y(0, 0)
-        turn_y(0, 1)
-        leaky(2, 0, 1)
-        quant_a(2, 0, 0)
-        leaky(2, 1, 0)
-        quant_a(2, 0, 1)
-        quant_x(6, 0, 2)
-        quant_a(2, 1, 0)
-        rates(2)
-        leaky(2, 1, 1)
-        for g in range(KG):
-            turn_pair(4, g)
-        quant_x(6, 1, 2)
-        quant_x(6, 2, 2)
-        planes(0)
-        quant_a(2, 1, 1)
-        banks = {2: [(0, 0), (0, 1), (0, 2), (0, 3)], 3: [(1, 0), (1, 1), (1, 2), (1, 3)]}
-        acts = {3: [(3, 0, 0)], 4: [(3, 1, 0)], 5: [(3, 0, 1)], 6: [(3, 1, 1)]}
-        for i in range(2, TILES):
-            if i > 2:
-                round_y(i - 1, NG - 1)
-            if i + 1 < TILES:
-                rates(i + 1)
-            if i == 2:
-                scale_y(2, 0)
-                quant_pair(4)
-            for fg, t in banks.get(i, []):
-                hidden_bank(3, fg, (t,))
-            turn_y(i - 1, 0)
-            turn_y(i - 1, 1)
-            for act in acts.get(i, []):
-                leaky(*act)
-            scales(i)
-            for act in acts.get(i, []):
-                quant_a(*act)
-            if i > 2:
-                planes(i - 2)
-        round_y(TILES - 1, NG - 1)
-        planes(TILES - 2)
-        turn_y(TILES - 1, 1)
-        planes(TILES - 1)
+        add_bias(2, 0)
+        add_bias(2, 1)
+        quant_a(1)
+        leaky(2)
+        last = TILES - 1
+        for s in range(last - 1):
+            if s > 0:
+                turn_y(s - 1, 0)
+                turn_y(s - 1, 1)
+            if s + 4 < TILES:
+                turn_x(s + 4)
+            if s + 2 < TILES:
+                turn_a(s + 2)
+            if s + 3 < TILES:
+                hidden(s + 3)
+            scale_y(s, 0)
+            if CASTS[s][0] != "V":
+                round_y(s, 0)
+            scale_y(s, 1)
+            store_y(s, 0, N)
+            if CASTS[s][1] != "V":
+                round_y(s, 1)
+            rates(s + 1)
+            if CASTS[s][0] == "V":
+                round_y(s, 0)
+            if s + 3 < TILES:
+                add_bias(s + 3, 0)
+                add_bias(s + 3, 1)
+            if CASTS[s][1] == "V":
+                round_y(s, 1)
+            if s + 2 < TILES:
+                quant_a(s + 2)
+            if s + 3 < TILES:
+                leaky(s + 3)
+            if s > 0:
+                quant_y(s - 1, range(NG))
+                store_planes(s - 1)
+            if s + 4 < TILES:
+                quant_x(s + 4)
+        def scale_last(n):
+            scale_y(last, n // 2, (n % 2) * BANK, (n % 2 + 1) * BANK)
+            store_y(last, n * BANK, (n + 1) * BANK)
+
+        rates(last)
+        scale_y(last - 1, 0)
+        scale_y(last - 1, 1)
+        store_y(last - 1, 0, N)
+        round_y(last - 1, 0, "S")
+        turn_y(last - 2, 0)
+        turn_y(last - 2, 1)
+        scale_last(0)
+        round_y(last - 1, 1, "V")
+        turn_y(last - 1, 0)
+        turn_y(last - 1, 1)
+        scale_last(1)
+        round_y(last, 0, "V", 0)
+        scale_last(2)
+        round_y(last, 0, "V", 1)
+        turn_y(last, 0)
+        scale_last(3)
+        round_y(last, 1, "V", 0)
+        quant_y(last - 2, range(2))
+        round_y(last, 1, "V", 1)
+        turn_y(last, 1)
+        quant_y(last - 2, range(2, NG))
+        store_planes(last - 2)
+        quant_y(last - 1, range(0, NG))
+        store_planes(last - 1)
+        quant_y(last, range(2))
+        store_codes(len(code_spans) - 1, slice(0, 2))
+        quant_y(last, range(2, NG))
+        store_codes(len(code_spans) - 1, slice(2, NG))
+        store_scales(1, nc.scalar)

@@ -26,7 +26,7 @@ KG, FG, NG = K // PASS, F // PASS, N // PASS
 TILES = M // P
 ROTATING_BANKS = 6
 THR_ROW = 32
-CASTS = ["SV"] * 10
+CASTS = ["GS"] * 10
 CY = ["SS"] * 10
 
 
@@ -45,8 +45,8 @@ def tile_impedance_ageing_rates_h1_kernel(
         w1_plane = keep.tile([P, KG, F], U8, name="w1_plane", align_bytes=64)
         w2_codes = keep.tile([P, FG, 2 * N], U8, name="w2_codes", align_bytes=64)
         w2_plane = keep.tile([P, FG, N], U8, name="w2_plane", align_bytes=64)
-        code_spans = [(0, 2), (2, 4), (4, 6), (6, 7), (7, 8), (8, 9), (9, 10)]
-        plane_spans = [(0, 7), (7, 10)]
+        code_spans = [(0, 2), (2, 4), (4, 6), (6, 7), (7, 8), (8, 10)]
+        plane_spans = [(0, 6), (6, 10)]
         y_codes = [keep.tile([P, NG, (b - a) * P], U32, name="y_codes%d" % a, align_bytes=64) for a, b in code_spans]
         y_plane = [keep.tile([P, NG, (b - a) * P], U8, name="y_plane%d" % a, align_bytes=64) for a, b in plane_spans]
         ident_f32 = keep.tile([P, P], F32, name="ident_f32", align_bytes=64)
@@ -75,10 +75,10 @@ def tile_impedance_ageing_rates_h1_kernel(
             nc.sync.dma_start(out=x_raw[:, i, :], in_=spectra[i * P : (i + 1) * P, :])
 
         def load_scales(plane, scales):
-            for q in range(4):
+            for r in range(4):
                 nc.sync.dma_start(
-                    out=plane[32 * q : 32 * q + 4, :, :].bitcast(I32),
-                    in_=scales[:, 4 * q : 4 * q + 4, :].rearrange("g r n -> r g n").bitcast(I32),
+                    out=plane[r:P:32, :, :].bitcast(I32),
+                    in_=scales[:, r:16:4, :].rearrange("g q n -> q g n").bitcast(I32),
                 )
 
         nc.vector.memset(w1_plane[:].rearrange("p g n -> p (g n)").bitcast(U32), 0)
@@ -91,9 +91,9 @@ def tile_impedance_ageing_rates_h1_kernel(
         load_x(0)
         nc.scalar.dma_start(out=bias_rows[0 : F // P, :], in_=b1.rearrange("(r c) -> r c", c=P))
         nc.scalar.activation(out=warm[:, 0:1], in_=warm[:, 8:9], func=ACT.Exp)
+        nc.sync.dma_start(out=w1_codes[:].bitcast(I32), in_=w1_words.rearrange("g p n -> p g n").bitcast(I32))
         load_scales(w1_plane, w1_scales)
         load_x(1)
-        nc.sync.dma_start(out=w1_codes[:].bitcast(I32), in_=w1_words.rearrange("g p n -> p g n").bitcast(I32))
         nc.gpsimd.dma_start(out=rows[0 : N // P, :], in_=base_rate.rearrange("(r c) -> r c", c=P))
         nc.gpsimd.dma_start(out=rows[THR_ROW : THR_ROW + TILES, :], in_=throughput.rearrange("(r c) -> r c", c=P))
         load_x(2)
@@ -235,7 +235,7 @@ def tile_impedance_ageing_rates_h1_kernel(
         def scale_y(i, half, lo=0, hi=HALF):
             if half == 0 and lo == 0:
                 y_f32[i] = work.tile([P, N], F32, name="y", bufs=3, align_bytes=64)
-                y_bf16[i] = work.tile([P, N], BF16, name="yb", bufs=3, align_bytes=64)
+                y_bf16[i] = work.tile([P, N], BF16, name="yb", bufs=4, align_bytes=64)
             nc.vector.scalar_tensor_tensor(
                 out=y_f32[i][:, half * HALF + lo : half * HALF + hi],
                 in0=growth[i, half][:, lo:hi],
@@ -258,7 +258,7 @@ def tile_impedance_ageing_rates_h1_kernel(
 
         def turn_y(i, half):
             if half == 0:
-                y_grouped[i] = work.tile([P, N], BF16, name="yg", bufs=3, align_bytes=64)
+                y_grouped[i] = work.tile([P, N], BF16, name="yg", bufs=4, align_bytes=64)
             bank = next_bank()
             words = y_bf16[i][:].bitcast(F32)
             for g in range(2):
@@ -289,10 +289,10 @@ def tile_impedance_ageing_rates_h1_kernel(
 
         def store_scales(j, queue):
             a, b = plane_spans[j]
-            for q in range(4):
+            for r in range(4):
                 queue.dma_start(
-                    out=out_2[:, 4 * q : 4 * q + 4, a * P : b * P].rearrange("g r m -> r g m").bitcast(I32),
-                    in_=y_plane[j][32 * q : 32 * q + 4, :, :].bitcast(I32),
+                    out=out_2[:, r:16:4, a * P : b * P].rearrange("g q m -> q g m").bitcast(I32),
+                    in_=y_plane[j][r:P:32, :, :].bitcast(I32),
                 )
 
         def store_planes(i):
@@ -333,7 +333,7 @@ def tile_impedance_ageing_rates_h1_kernel(
         quant_a(1)
         leaky(2)
         last = TILES - 1
-        for s in range(last - 1):
+        for s in range(last - 2):
             if s > 0:
                 turn_y(s - 1, 0)
                 turn_y(s - 1, 1)
@@ -371,31 +371,40 @@ def tile_impedance_ageing_rates_h1_kernel(
             scale_y(last, n // 2, (n % 2) * BANK, (n % 2 + 1) * BANK)
             store_y(last, n * BANK, (n + 1) * BANK)
 
+        turn_a(last)
+        turn_y(last - 3, 0)
+        turn_y(last - 3, 1)
+        rates(last - 1)
+        scale_y(last - 2, 0)
+        quant_a(last)
         rates(last)
-        scale_y(last - 1, 0)
-        scale_y(last - 1, 1)
-        store_y(last - 1, 0, N)
-        round_y(last - 1, 0, "S")
-        turn_y(last - 2, 0)
-        turn_y(last - 2, 1)
+        round_y(last - 2, 0, "G")
+        store_y(last - 2, 0, HALF)
+        scale_y(last - 2, 1)
+        store_y(last - 2, HALF, N)
+        quant_y(last - 3, range(NG))
+        store_planes(last - 3)
+        round_y(last - 2, 1, "G")
+        for half in range(2):
+            scale_y(last - 1, half)
+            round_y(last - 1, half, "G")
+            store_y(last - 1, half * HALF, (half + 1) * HALF)
+        for i in range(last - 2, last):
+            turn_y(i, 0)
+            turn_y(i, 1)
         scale_last(0)
-        round_y(last - 1, 1, "V")
-        turn_y(last - 1, 0)
-        turn_y(last - 1, 1)
         scale_last(1)
-        round_y(last, 0, "V", 0)
         scale_last(2)
+        scale_last(3)
+        round_y(last, 0, "V", 0)
         round_y(last, 0, "V", 1)
         turn_y(last, 0)
-        scale_last(3)
         round_y(last, 1, "V", 0)
-        quant_y(last - 2, range(2))
         round_y(last, 1, "V", 1)
         turn_y(last, 1)
-        quant_y(last - 2, range(2, NG))
-        store_planes(last - 2)
-        quant_y(last - 1, range(0, NG))
-        store_planes(last - 1)
+        for i in range(last - 2, last):
+            quant_y(i, range(NG))
+            store_planes(i)
         quant_y(last, range(2))
         store_codes(len(code_spans) - 1, slice(0, 2))
         quant_y(last, range(2, NG))

@@ -26,7 +26,7 @@ KG, FG, NG = K // PASS, F // PASS, N // PASS
 TILES = M // P
 ROTATING_BANKS = 6
 THR_ROW = 32
-CASTS = ["GS"] * 10
+CASTS = ["VS"] * 10
 CY = ["SS"] * 10
 
 
@@ -46,6 +46,7 @@ def tile_impedance_ageing_rates_h1_kernel(
         w2_codes = keep.tile([P, FG, 2 * N], U8, name="w2_codes", align_bytes=64)
         w2_plane = keep.tile([P, FG, N], U8, name="w2_plane", align_bytes=64)
         code_spans = [(0, 2), (2, 4), (4, 6), (6, 7), (7, 8), (8, 10)]
+        quant_spans = [(0, 2), (2, 4), (4, 6), (6, 7), (7, 8), (8, 9), (9, 10)]
         plane_spans = [(0, 6), (6, 10)]
         y_codes = [keep.tile([P, NG, (b - a) * P], U32, name="y_codes%d" % a, align_bytes=64) for a, b in code_spans]
         y_plane = [keep.tile([P, NG, (b - a) * P], U8, name="y_plane%d" % a, align_bytes=64) for a, b in plane_spans]
@@ -59,11 +60,6 @@ def tile_impedance_ageing_rates_h1_kernel(
         bias_wide = keep.tile([P, F], BF16, name="bias_wide", align_bytes=64)
         warm = keep.tile([P, 16], F32, name="warm", align_bytes=64)
         base_wide = [psum.tile([P, HALF], BF16, name="base_wide%d" % j) for j in range(2)]
-
-        def window(tiles, spans, i, n):
-            j = [a <= i < b for a, b in spans].index(True)
-            lo = (i - spans[j][0]) * P
-            return tiles[j][:, n, lo : lo + P]
 
         bank_count = [0]
 
@@ -81,19 +77,19 @@ def tile_impedance_ageing_rates_h1_kernel(
                     in_=scales[:, r:16:4, :].rearrange("g q n -> q g n").bitcast(I32),
                 )
 
-        nc.vector.memset(w1_plane[:].rearrange("p g n -> p (g n)").bitcast(U32), 0)
         nc.vector.memset(bias_rows[:], 0.0)
+        nc.vector.memset(w1_plane[:].rearrange("p g n -> p (g n)").bitcast(U32), 0)
         nc.vector.memset(warm[:], 0.0)
         nc.vector.memset(rows[:], 0.0)
         nc.vector.memset(w2_plane[:].rearrange("p g n -> p (g n)").bitcast(U32), 0)
-        make_identity(nc, ident_f32[:])
         make_identity(nc, ident_bf16[:])
+        make_identity(nc, ident_f32[:])
         load_x(0)
         nc.scalar.dma_start(out=bias_rows[0 : F // P, :], in_=b1.rearrange("(r c) -> r c", c=P))
         nc.scalar.activation(out=warm[:, 0:1], in_=warm[:, 8:9], func=ACT.Exp)
+        load_x(1)
         nc.sync.dma_start(out=w1_codes[:].bitcast(I32), in_=w1_words.rearrange("g p n -> p g n").bitcast(I32))
         load_scales(w1_plane, w1_scales)
-        load_x(1)
         nc.gpsimd.dma_start(out=rows[0 : N // P, :], in_=base_rate.rearrange("(r c) -> r c", c=P))
         nc.gpsimd.dma_start(out=rows[THR_ROW : THR_ROW + TILES, :], in_=throughput.rearrange("(r c) -> r c", c=P))
         load_x(2)
@@ -104,23 +100,38 @@ def tile_impedance_ageing_rates_h1_kernel(
             load_x(i)
 
         def turn_bias():
-            turned = next_bank()[:].bitcast(BF16)[:, 0:P]
-            nc.tensor.transpose(turned, bias_rows[:], ident_bf16[:])
-            nc.vector.tensor_copy(out=bias_cols[:], in_=turned[:, 0 : F // P])
+            flipped = next_bank()[:].bitcast(BF16)[:, 0:P]
+            nc.tensor.transpose(flipped, bias_rows[:], ident_bf16[:])
+            nc.vector.tensor_copy(out=bias_cols[:], in_=flipped[:, 0 : F // P])
 
         def turn_rows():
-            turned = next_bank()[:].bitcast(BF16)[:, 0:P]
-            nc.tensor.transpose(turned, rows[:], ident_bf16[:])
-            nc.vector.tensor_copy(out=base_cols[:], in_=turned[:, 0 : N // P])
-            nc.vector.tensor_copy(out=thr[:], in_=turned[:, THR_ROW : THR_ROW + TILES])
+            flipped = next_bank()[:].bitcast(BF16)[:, 0:P]
+            nc.tensor.transpose(flipped, rows[:], ident_bf16[:])
+            nc.vector.tensor_copy(out=base_cols[:], in_=flipped[:, 0 : N // P])
+            nc.vector.tensor_copy(out=thr[:], in_=flipped[:, THR_ROW : THR_ROW + TILES])
+
+        rows_bank = []
+
+        def turn_rows_pe():
+            rows_bank.append(next_bank()[:].bitcast(BF16)[:, 0:P])
+            nc.tensor.transpose(rows_bank[0], rows[:], ident_bf16[:])
+
+        def turn_rows_copy():
+            nc.vector.tensor_copy(out=base_cols[:], in_=rows_bank[0][:, 0 : N // P])
+            nc.vector.tensor_copy(out=thr[:], in_=rows_bank[0][:, THR_ROW : THR_ROW + TILES])
 
         def spread(wide, cols, first):
             for c in range(HALF // P):
                 nc.tensor.transpose(wide[:, c * P : (c + 1) * P], cols[:, first + c : first + c + 1].to_broadcast([P, P]), ident_bf16[:])
 
+        bias_bank = []
+
         def spread_bias():
-            wide = next_bank()[:].bitcast(BF16)
-            spread(wide, bias_cols, 0)
+            bias_bank.append(next_bank()[:].bitcast(BF16))
+            spread(bias_bank[0], bias_cols, 0)
+
+        def copy_bias():
+            wide = bias_bank[0]
             for fg in range(FG):
                 nc.vector.tensor_copy(
                     out=bias_wide[:, fg * BANK : (fg + 1) * BANK].rearrange("p (u m e) -> p u m e", u=2, e=2),
@@ -142,30 +153,43 @@ def tile_impedance_ageing_rates_h1_kernel(
                 bank[:, 0 : groups * 2 * P].rearrange("p (g u m) -> p g m u", g=groups, u=2),
             )
 
-        x_grouped, x_mx, h_banks, h_f32, a_bf16, a_grouped, a_mx = {}, {}, {}, {}, {}, {}, {}
+        turned, x_mx, h_banks, h_f32, a_bf16, a_mx = {}, {}, {}, {}, {}, {}
         growth, y_f32, y_bf16, y_banks, y_grouped = {}, {}, {}, {}, {}
 
-        def turn_x(i):
-            words = x_raw[:, i, :].bitcast(F32)
-            x_grouped[i] = work.tile([P, K], BF16, name="xg", bufs=3, align_bytes=64)
-            for first, groups in ((0, 2), (2, 1)):
+        def turn(xi, ai):
+            sources = []
+            if xi is not None:
+                words = x_raw[:, xi, :].bitcast(F32)
+                sources += [[words[:, 2 * P * g + u : 2 * P * (g + 1) : 2] for u in range(2)] for g in range(KG)]
+            if ai is not None:
+                words = a_bf16[ai][:].bitcast(F32)
+                sources += [[words[:, (2 * g + u) * P : (2 * g + u + 1) * P] for u in range(2)] for g in range(FG)]
+            grouped = work.tile([P, K + F], BF16, name="grouped", bufs=3, align_bytes=64)
+            for first in range(0, len(sources), 2):
                 bank = next_bank()
-                for g in range(groups):
+                groups = sources[first : first + 2]
+                for g, pair in enumerate(groups):
                     for u in range(2):
-                        lo = 2 * P * (first + g)
-                        col = (2 * g + u) * P
-                        nc.tensor.transpose(bank[:, col : col + P], words[:, lo + u : lo + 2 * P : 2], ident_f32[:])
-                interleave("S", x_grouped[i][:, first * PASS : (first + groups) * PASS], bank, groups)
+                        nc.tensor.transpose(bank[:, (2 * g + u) * P : (2 * g + u + 1) * P], pair[u], ident_f32[:])
+                interleave("S", grouped[:, first * PASS : (first + len(groups)) * PASS], bank, len(groups))
+            turned[xi, ai] = (grouped, len(sources))
 
-        def quant_x(i):
-            codes = work.tile([P, KG * P], U32, name="xq", bufs=3, align_bytes=64)
-            plane = work.tile([P, KG * P], U8, name="xs", bufs=3, align_bytes=64)
-            for first, groups in ((0, 2), (2, 1)):
-                span = slice(first * P, (first + groups) * P)
-                nc.vector.quantize_mx(
-                    out=codes[:, span].bitcast(FP8X4), scales=plane[:, span], in_=x_grouped[i][:, first * PASS : (first + groups) * PASS]
-                )
-            x_mx[i] = (codes, plane)
+        def quant(xi, ai):
+            grouped, count = turned[xi, ai]
+            codes = work.tile([P, (KG + FG) * P], U32, name="codes", bufs=4, align_bytes=64)
+            plane = work.tile([P, (KG + FG) * P], U8, name="plane", bufs=4, align_bytes=64)
+            wide = 4 if count >= 4 else 2
+            for first, stop in ((0, wide), (wide, count)):
+                if stop > first:
+                    nc.vector.quantize_mx(
+                        out=codes[:, first * P : stop * P].bitcast(FP8X4),
+                        scales=plane[:, first * P : stop * P],
+                        in_=grouped[:, first * PASS : stop * PASS],
+                    )
+            if xi is not None:
+                x_mx[xi] = (codes[:, 0 : KG * P], plane[:, 0 : KG * P])
+            if ai is not None:
+                a_mx[ai] = (codes[:, (count - FG) * P : count * P], plane[:, (count - FG) * P : count * P])
 
         def hidden(i):
             codes, plane = x_mx[i]
@@ -199,20 +223,6 @@ def tile_impedance_ageing_rates_h1_kernel(
             nc.vector.scalar_tensor_tensor(
                 out=a_bf16[i][:], in0=h_f32[i][:], scalar=SLOPE, in1=h_f32[i][:], op0=ALU.mult, op1=ALU.max
             )
-
-        def turn_a(i):
-            bank = next_bank()
-            words = a_bf16[i][:].bitcast(F32)
-            for j in range(4):
-                nc.tensor.transpose(bank[:, j * P : (j + 1) * P], words[:, j * P : (j + 1) * P], ident_f32[:])
-            a_grouped[i] = work.tile([P, F], BF16, name="ag", bufs=2, align_bytes=64)
-            interleave("S", a_grouped[i][:], bank, FG)
-
-        def quant_a(i):
-            codes = work.tile([P, FG * P], U32, name="aq", bufs=3, align_bytes=64)
-            plane = work.tile([P, FG * P], U8, name="as", bufs=3, align_bytes=64)
-            nc.vector.quantize_mx(out=codes[:].bitcast(FP8X4), scales=plane[:], in_=a_grouped[i][:])
-            a_mx[i] = (codes, plane)
 
         def rates(i):
             codes, plane = a_mx[i]
@@ -256,28 +266,36 @@ def tile_impedance_ageing_rates_h1_kernel(
         def store_y(i, lo, hi):
             nc.sync.dma_start(out=out_0[i * P : (i + 1) * P, lo:hi], in_=y_f32[i][:, lo:hi])
 
+        def span_of(spans, i):
+            return [a <= i < b for a, b in spans].index(True)
+
         def turn_y(i, half):
-            if half == 0:
-                y_grouped[i] = work.tile([P, N], BF16, name="yg", bufs=4, align_bytes=64)
+            j = span_of(quant_spans, i)
+            a, b = quant_spans[j]
+            if half == 0 and i == a:
+                y_grouped[j] = work.tile([P, NG, (b - a) * PASS], BF16, name="yg", bufs=3, align_bytes=64)
             bank = next_bank()
             words = y_bf16[i][:].bitcast(F32)
             for g in range(2):
                 for u in range(2):
                     lo = half * BANK + (2 * u + g) * P
                     nc.tensor.transpose(bank[:, (2 * g + u) * P : (2 * g + u + 1) * P], words[:, lo : lo + P], ident_f32[:])
-            y_banks[i, half] = bank
-            if CY[i][half] == "S":
-                drain_y(i, half)
+            nc.scalar.copy(
+                out=y_grouped[j][:, 2 * half : 2 * half + 2, (i - a) * PASS : (i - a + 1) * PASS].bitcast(F32).rearrange("p g (m u) -> p g m u", u=2),
+                in_=bank[:].rearrange("p (g u m) -> p g m u", g=2, u=2),
+            )
 
-        def drain_y(i, half):
-            interleave(CY[i][half], y_grouped[i][:, half * HALF : (half + 1) * HALF], y_banks[i, half], 2)
+        def window(tiles, spans, a, b, n):
+            j = span_of(spans, a)
+            return tiles[j][:, n, (a - spans[j][0]) * P : (b - spans[j][0]) * P]
 
-        def quant_y(i, groups):
+        def quant_y(j, groups):
+            a, b = quant_spans[j]
             for n in groups:
                 nc.vector.quantize_mx(
-                    out=window(y_codes, code_spans, i, n).bitcast(FP8X4),
-                    scales=window(y_plane, plane_spans, i, n),
-                    in_=y_grouped[i][:, n * BANK : (n + 1) * BANK],
+                    out=window(y_codes, code_spans, a, b, n).bitcast(FP8X4),
+                    scales=window(y_plane, plane_spans, a, b, n),
+                    in_=y_grouped[j][:, n, :],
                 )
 
         def store_codes(j, groups):
@@ -302,111 +320,108 @@ def tile_impedance_ageing_rates_h1_kernel(
             if i + 1 == plane_spans[0][1]:
                 store_scales(0, nc.sync)
 
-        turn_x(0)
         turn_bias()
-        quant_x(0)
+        turn(0, None)
         spread_bias()
+        quant(0, None)
+        turn(1, None)
+        copy_bias()
+        quant(1, None)
         hidden(0)
-        turn_x(1)
-        turn_x(2)
+        turn(2, None)
+        turn_rows_pe()
+        hidden(1)
         add_bias(0, 0)
         add_bias(0, 1)
-        quant_x(1)
-        turn_rows()
-        hidden(1)
+        turn_rows_copy()
         leaky(0)
-        quant_x(2)
+        quant(2, None)
         add_bias(1, 0)
         add_bias(1, 1)
-        turn_x(3)
-        turn_a(0)
         spread(base_wide[0], base_cols, 0)
+        turn(3, 0)
         hidden(2)
         leaky(1)
-        quant_a(0)
-        quant_x(3)
-        turn_a(1)
+        quant(3, 0)
+        turn(None, 1)
         spread(base_wide[1], base_cols, HALF // P)
         rates(0)
         add_bias(2, 0)
         add_bias(2, 1)
-        quant_a(1)
+        quant(None, 1)
         leaky(2)
         last = TILES - 1
         for s in range(last - 2):
             if s > 0:
                 turn_y(s - 1, 0)
                 turn_y(s - 1, 1)
-            if s + 4 < TILES:
-                turn_x(s + 4)
-            if s + 2 < TILES:
-                turn_a(s + 2)
-            if s + 3 < TILES:
-                hidden(s + 3)
+            hidden(s + 3)
             scale_y(s, 0)
-            if CASTS[s][0] != "V":
-                round_y(s, 0)
+            round_y(s, 0, "G")
             scale_y(s, 1)
             store_y(s, 0, N)
-            if CASTS[s][1] != "V":
-                round_y(s, 1)
+            round_y(s, 1, "G", 0)
+            round_y(s, 1, "S", 1)
+            ahead = (s + 4 if s + 4 < TILES else None, s + 2)
+            turn(*ahead)
             rates(s + 1)
-            if CASTS[s][0] == "V":
-                round_y(s, 0)
-            if s + 3 < TILES:
-                add_bias(s + 3, 0)
-                add_bias(s + 3, 1)
-            if CASTS[s][1] == "V":
-                round_y(s, 1)
-            if s + 2 < TILES:
-                quant_a(s + 2)
-            if s + 3 < TILES:
+            add_bias(s + 3, 0)
+            add_bias(s + 3, 1)
+            if s == last - 3:
+                quant(*ahead)
                 leaky(s + 3)
-            if s > 0:
-                quant_y(s - 1, range(NG))
-                store_planes(s - 1)
-            if s + 4 < TILES:
-                quant_x(s + 4)
-        def scale_last(n):
-            scale_y(last, n // 2, (n % 2) * BANK, (n % 2 + 1) * BANK)
-            store_y(last, n * BANK, (n + 1) * BANK)
-
-        turn_a(last)
-        turn_y(last - 3, 0)
-        turn_y(last - 3, 1)
-        rates(last - 1)
-        scale_y(last - 2, 0)
-        quant_a(last)
+            if s >= 2:
+                quant_y(s // 2 - 1, range(2 * (s % 2), 2 * (s % 2) + 2))
+                if s % 2 == 1:
+                    store_planes(s - 2)
+            if s < last - 3:
+                leaky(s + 3)
+                quant(*ahead)
+        turn(None, last)
+        turn_y(6, 0)
+        turn_y(6, 1)
+        rates(8)
+        scale_y(7, 0)
+        quant(None, last)
         rates(last)
-        round_y(last - 2, 0, "G")
-        store_y(last - 2, 0, HALF)
-        scale_y(last - 2, 1)
-        store_y(last - 2, HALF, N)
-        quant_y(last - 3, range(NG))
-        store_planes(last - 3)
-        round_y(last - 2, 1, "G")
-        for half in range(2):
-            scale_y(last - 1, half)
-            round_y(last - 1, half, "G")
-            store_y(last - 1, half * HALF, (half + 1) * HALF)
-        for i in range(last - 2, last):
-            turn_y(i, 0)
-            turn_y(i, 1)
-        scale_last(0)
-        scale_last(1)
-        scale_last(2)
-        scale_last(3)
-        round_y(last, 0, "V", 0)
-        round_y(last, 0, "V", 1)
-        turn_y(last, 0)
-        round_y(last, 1, "V", 0)
-        round_y(last, 1, "V", 1)
-        turn_y(last, 1)
-        for i in range(last - 2, last):
-            quant_y(i, range(NG))
-            store_planes(i)
-        quant_y(last, range(2))
+        store_y(7, 0, HALF)
+        round_y(7, 0, "G")
+        scale_y(7, 1)
+        store_y(7, HALF, N)
+        quant_y(2, range(2, NG))
+        store_planes(5)
+        quant_y(3, range(NG))
+        store_planes(6)
+        round_y(7, 1, "G")
+        turn_y(7, 0)
+        turn_y(7, 1)
+        scale_y(8, 0)
+        store_y(8, 0 * HALF, 1 * HALF)
+        round_y(8, 0, "G")
+        turn_y(8, 0)
+        scale_y(8, 1)
+        store_y(8, 1 * HALF, 2 * HALF)
+        round_y(8, 1, "G")
+        turn_y(8, 1)
+        scale_y(9, 0, 0 * BANK, 1 * BANK)
+        store_y(9, 0 * BANK, 1 * BANK)
+        scale_y(9, 0, 1 * BANK, 2 * BANK)
+        store_y(9, 1 * BANK, 2 * BANK)
+        scale_y(9, 1, 0 * BANK, 1 * BANK)
+        store_y(9, 2 * BANK, 3 * BANK)
+        scale_y(9, 1, 1 * BANK, 2 * BANK)
+        store_y(9, 3 * BANK, 4 * BANK)
+        round_y(9, 0, "V", 0)
+        round_y(9, 0, "V", 1)
+        turn_y(9, 0)
+        round_y(9, 1, "V", 0)
+        round_y(9, 1, "V", 1)
+        turn_y(9, 1)
+        quant_y(4, range(NG))
+        store_planes(7)
+        quant_y(5, range(NG))
+        quant_y(6, range(2))
         store_codes(len(code_spans) - 1, slice(0, 2))
-        quant_y(last, range(2, NG))
+        quant_y(6, range(2, NG))
         store_codes(len(code_spans) - 1, slice(2, NG))
         store_scales(1, nc.scalar)

@@ -19,15 +19,16 @@ ALU = mybir.AluOpType
 
 P = 128
 PACK = 4
-PASS = P * PACK
-BANK = 512
+GROUP = P * PACK
 HALF = N // 2
-KG, FG, NG = K // PASS, F // PASS, N // PASS
+KG, FG, NG = K // GROUP, F // GROUP, N // GROUP
 TILES = M // P
+LAST = TILES - 1
 ROTATING_BANKS = 6
+SPREAD = HALF // P
 THR_ROW = 32
-CASTS = ["VS"] * 10
-CY = ["SS"] * 10
+CODE_SPANS = [(0, 2), (2, 4), (4, 6), (6, 7), (7, 8), (8, 10)]
+PLANE_SPANS = [(0, 6), (6, 10)]
 
 
 def tile_impedance_ageing_rates_h1_kernel(
@@ -41,34 +42,34 @@ def tile_impedance_ageing_rates_h1_kernel(
         ctx.enter_context(tc.manual_schedule())
 
         x_raw = keep.tile([P, TILES, K], BF16, name="x_raw", align_bytes=64)
-        w1_codes = keep.tile([P, KG, 2 * F], U8, name="w1_codes", align_bytes=64)
+        w1_codes = keep.tile([P, FG, KG, 2 * GROUP], U8, name="w1_codes", align_bytes=64)
         w1_plane = keep.tile([P, KG, F], U8, name="w1_plane", align_bytes=64)
         w2_codes = keep.tile([P, FG, 2 * N], U8, name="w2_codes", align_bytes=64)
         w2_plane = keep.tile([P, FG, N], U8, name="w2_plane", align_bytes=64)
-        code_spans = [(0, 2), (2, 4), (4, 6), (6, 7), (7, 8), (8, 10)]
-        quant_spans = [(0, 2), (2, 4), (4, 6), (6, 7), (7, 8), (8, 9), (9, 10)]
-        plane_spans = [(0, 6), (6, 10)]
-        y_codes = [keep.tile([P, NG, (b - a) * P], U32, name="y_codes%d" % a, align_bytes=64) for a, b in code_spans]
-        y_plane = [keep.tile([P, NG, (b - a) * P], U8, name="y_plane%d" % a, align_bytes=64) for a, b in plane_spans]
+        y_codes = [keep.tile([P, NG, (b - a) * P], U32, name="y_codes%d" % a, align_bytes=64) for a, b in CODE_SPANS]
+        y_plane = [keep.tile([P, NG, (b - a) * P], U8, name="y_plane%d" % a, align_bytes=64) for a, b in PLANE_SPANS]
         ident_f32 = keep.tile([P, P], F32, name="ident_f32", align_bytes=64)
         ident_bf16 = keep.tile([P, P], BF16, name="ident_bf16", align_bytes=64)
-        bias_rows = keep.tile([P, P], BF16, name="bias_rows", align_bytes=64)
-        bias_cols = keep.tile([P, F // P], BF16, name="bias_cols", align_bytes=64)
+        bias_cols = keep.tile([P, SPREAD], BF16, name="bias_cols", align_bytes=64)
+        bias_wide = keep.tile([P, F], BF16, name="bias_wide", align_bytes=64)
         rows = keep.tile([P, P], BF16, name="rows", align_bytes=64)
         base_cols = keep.tile([P, N // P], BF16, name="base_cols", align_bytes=64)
         thr = keep.tile([P, TILES], F32, name="thr", align_bytes=64)
-        bias_wide = keep.tile([P, F], BF16, name="bias_wide", align_bytes=64)
-        warm = keep.tile([P, 16], F32, name="warm", align_bytes=64)
-        base_wide = [psum.tile([P, HALF], BF16, name="base_wide%d" % j) for j in range(2)]
+        base_wide = [psum.tile([P, HALF], BF16, name="base_wide%d" % half) for half in range(2)]
 
-        bank_count = [0]
+        banks_taken = [0]
 
         def next_bank():
-            bank_count[0] += 1
-            return psum.tile([P, BANK], F32, name="bank%d" % (bank_count[0] % ROTATING_BANKS))
+            banks_taken[0] += 1
+            return psum.tile([P, GROUP], F32, name="bank%d" % (banks_taken[0] % ROTATING_BANKS))
+
 
         def load_x(i):
             nc.sync.dma_start(out=x_raw[:, i, :], in_=spectra[i * P : (i + 1) * P, :])
+
+        def load_w1(fg):
+            columns = w1_words[:, :, fg * 2 * GROUP : (fg + 1) * 2 * GROUP]
+            nc.sync.dma_start(out=w1_codes[:, fg].bitcast(I32), in_=columns.rearrange("g p n -> p g n").bitcast(I32))
 
         def load_scales(plane, scales):
             for r in range(4):
@@ -77,19 +78,17 @@ def tile_impedance_ageing_rates_h1_kernel(
                     in_=scales[:, r:16:4, :].rearrange("g q n -> q g n").bitcast(I32),
                 )
 
-        nc.vector.memset(bias_rows[:], 0.0)
         nc.vector.memset(w1_plane[:].rearrange("p g n -> p (g n)").bitcast(U32), 0)
-        nc.vector.memset(warm[:], 0.0)
         nc.vector.memset(rows[:], 0.0)
         nc.vector.memset(w2_plane[:].rearrange("p g n -> p (g n)").bitcast(U32), 0)
-        make_identity(nc, ident_bf16[:])
         make_identity(nc, ident_f32[:])
+        make_identity(nc, ident_bf16[:])
         load_x(0)
-        nc.scalar.dma_start(out=bias_rows[0 : F // P, :], in_=b1.rearrange("(r c) -> r c", c=P))
-        nc.scalar.activation(out=warm[:, 0:1], in_=warm[:, 8:9], func=ACT.Exp)
-        load_x(1)
-        nc.sync.dma_start(out=w1_codes[:].bitcast(I32), in_=w1_words.rearrange("g p n -> p g n").bitcast(I32))
+        nc.scalar.dma_start(out=bias_cols[:], in_=b1.rearrange("(n c) -> n c", c=SPREAD))
+        load_w1(0)
         load_scales(w1_plane, w1_scales)
+        load_x(1)
+        load_w1(1)
         nc.gpsimd.dma_start(out=rows[0 : N // P, :], in_=base_rate.rearrange("(r c) -> r c", c=P))
         nc.gpsimd.dma_start(out=rows[THR_ROW : THR_ROW + TILES, :], in_=throughput.rearrange("(r c) -> r c", c=P))
         load_x(2)
@@ -99,83 +98,55 @@ def tile_impedance_ageing_rates_h1_kernel(
         for i in range(4, TILES):
             load_x(i)
 
-        def turn_bias():
-            flipped = next_bank()[:].bitcast(BF16)[:, 0:P]
-            nc.tensor.transpose(flipped, bias_rows[:], ident_bf16[:])
-            nc.vector.tensor_copy(out=bias_cols[:], in_=flipped[:, 0 : F // P])
-
-        def turn_rows():
-            flipped = next_bank()[:].bitcast(BF16)[:, 0:P]
-            nc.tensor.transpose(flipped, rows[:], ident_bf16[:])
-            nc.vector.tensor_copy(out=base_cols[:], in_=flipped[:, 0 : N // P])
-            nc.vector.tensor_copy(out=thr[:], in_=flipped[:, THR_ROW : THR_ROW + TILES])
-
-        rows_bank = []
-
-        def turn_rows_pe():
-            rows_bank.append(next_bank()[:].bitcast(BF16)[:, 0:P])
-            nc.tensor.transpose(rows_bank[0], rows[:], ident_bf16[:])
-
-        def turn_rows_copy():
-            nc.vector.tensor_copy(out=base_cols[:], in_=rows_bank[0][:, 0 : N // P])
-            nc.vector.tensor_copy(out=thr[:], in_=rows_bank[0][:, THR_ROW : THR_ROW + TILES])
 
         def spread(wide, cols, first):
-            for c in range(HALF // P):
-                nc.tensor.transpose(wide[:, c * P : (c + 1) * P], cols[:, first + c : first + c + 1].to_broadcast([P, P]), ident_bf16[:])
-
-        bias_bank = []
+            for c in range(SPREAD):
+                column = cols[:, first + c : first + c + 1].to_broadcast([P, P])
+                nc.tensor.transpose(wide[:, c * P : (c + 1) * P], column, ident_bf16[:])
 
         def spread_bias():
-            bias_bank.append(next_bank()[:].bitcast(BF16))
-            spread(bias_bank[0], bias_cols, 0)
-
-        def copy_bias():
-            wide = bias_bank[0]
+            wide = next_bank()[:].bitcast(BF16)
+            spread(wide, bias_cols, 0)
+            src = wide.rearrange("p (b u e g a) -> p g u a b e", b=2, u=2, e=2, g=FG)
+            dst = bias_wide[:].rearrange("p (g u a b e) -> p g u a b e", b=2, u=2, e=2, g=FG)
             for fg in range(FG):
-                nc.vector.tensor_copy(
-                    out=bias_wide[:, fg * BANK : (fg + 1) * BANK].rearrange("p (u m e) -> p u m e", u=2, e=2),
-                    in_=wide[:, fg * BANK : (fg + 1) * BANK].rearrange("p (m u e) -> p u m e", u=2, e=2),
-                )
+                for u in range(2):
+                    nc.vector.tensor_copy(out=dst[:, fg, u], in_=src[:, fg, u])
 
-        def copy_on(engine, out, in_):
-            if engine == "S":
-                nc.scalar.copy(out=out, in_=in_)
-            elif engine == "V":
-                nc.vector.tensor_copy(out=out, in_=in_)
-            else:
-                nc.gpsimd.tensor_scalar(out=out, in0=in_, scalar1=1.0, scalar2=0.0, op0=ALU.mult, op1=ALU.add)
+        def turn_rows():
+            columns = next_bank()[:].bitcast(BF16)[:, 0:P]
+            nc.tensor.transpose(columns, rows[:], ident_bf16[:])
+            nc.vector.tensor_copy(out=base_cols[:], in_=columns[:, 0 : N // P])
+            nc.scalar.activation(out=thr[:], in_=columns[:, THR_ROW : THR_ROW + TILES], func=ACT.Identity)
 
-        def interleave(engine, grouped, bank, groups):
-            copy_on(
-                engine,
-                grouped.bitcast(F32).rearrange("p (g m u) -> p g m u", g=groups, u=2),
-                bank[:, 0 : groups * 2 * P].rearrange("p (g u m) -> p g m u", g=groups, u=2),
-            )
 
-        turned, x_mx, h_banks, h_f32, a_bf16, a_mx = {}, {}, {}, {}, {}, {}
-        growth, y_f32, y_bf16, y_banks, y_grouped = {}, {}, {}, {}, {}
+        grouped, x_mx, h_banks, h_f32, a_bf16, a_mx = {}, {}, {}, {}, {}, {}
 
         def turn(xi, ai):
-            sources = []
+            pairs = []
             if xi is not None:
                 words = x_raw[:, xi, :].bitcast(F32)
-                sources += [[words[:, 2 * P * g + u : 2 * P * (g + 1) : 2] for u in range(2)] for g in range(KG)]
+                pairs += [[words[:, 2 * P * g + u : 2 * P * (g + 1) : 2] for u in range(2)] for g in range(KG)]
             if ai is not None:
                 words = a_bf16[ai][:].bitcast(F32)
-                sources += [[words[:, (2 * g + u) * P : (2 * g + u + 1) * P] for u in range(2)] for g in range(FG)]
-            grouped = work.tile([P, K + F], BF16, name="grouped", bufs=3, align_bytes=64)
-            for first in range(0, len(sources), 2):
+                pairs += [[words[:, (2 * g + u) * P : (2 * g + u + 1) * P] for u in range(2)] for g in range(FG)]
+            staged = work.tile([P, K + F], BF16, name="staged", bufs=3, align_bytes=64)
+            for first in range(0, len(pairs), 2):
                 bank = next_bank()
-                groups = sources[first : first + 2]
-                for g, pair in enumerate(groups):
+                in_bank = pairs[first : first + 2]
+                count = len(in_bank)
+                for g in range(count):
                     for u in range(2):
-                        nc.tensor.transpose(bank[:, (2 * g + u) * P : (2 * g + u + 1) * P], pair[u], ident_f32[:])
-                interleave("S", grouped[:, first * PASS : (first + len(groups)) * PASS], bank, len(groups))
-            turned[xi, ai] = (grouped, len(sources))
+                        nc.tensor.transpose(bank[:, (2 * g + u) * P : (2 * g + u + 1) * P], in_bank[g][u], ident_f32[:])
+                words_out = staged[:, first * GROUP : (first + count) * GROUP].bitcast(F32)
+                nc.scalar.copy(
+                    out=words_out.rearrange("p (g m u) -> p g m u", g=count, u=2),
+                    in_=bank[:, 0 : count * 2 * P].rearrange("p (g u m) -> p g m u", g=count, u=2),
+                )
+            grouped[xi, ai] = (staged, len(pairs))
 
         def quant(xi, ai):
-            grouped, count = turned[xi, ai]
+            staged, count = grouped[xi, ai]
             codes = work.tile([P, (KG + FG) * P], U32, name="codes", bufs=4, align_bytes=64)
             plane = work.tile([P, (KG + FG) * P], U8, name="plane", bufs=4, align_bytes=64)
             wide = 4 if count >= 4 else 2
@@ -184,7 +155,7 @@ def tile_impedance_ageing_rates_h1_kernel(
                     nc.vector.quantize_mx(
                         out=codes[:, first * P : stop * P].bitcast(FP8X4),
                         scales=plane[:, first * P : stop * P],
-                        in_=grouped[:, first * PASS : stop * PASS],
+                        in_=staged[:, first * GROUP : stop * GROUP],
                     )
             if xi is not None:
                 x_mx[xi] = (codes[:, 0 : KG * P], plane[:, 0 : KG * P])
@@ -200,228 +171,213 @@ def tile_impedance_ageing_rates_h1_kernel(
                         out=bank[:],
                         lhsT=codes[:, g * P : (g + 1) * P].bitcast(FP8X4),
                         lhsT_scale=plane[:, g * P : (g + 1) * P],
-                        rhs=w1_codes[:, g, fg * 2 * BANK : (fg + 1) * 2 * BANK].bitcast(FP4X4),
-                        rhs_scale=w1_plane[:, g, fg * BANK : (fg + 1) * BANK],
+                        rhs=w1_codes[:, fg, g, :].bitcast(FP4X4),
+                        rhs_scale=w1_plane[:, g, fg * GROUP : (fg + 1) * GROUP],
                         start=(g == 0),
                         stop=(g == KG - 1),
                     )
                 h_banks[i, fg] = bank
 
-        def add_bias(i, fg):
-            if fg == 0:
-                h_f32[i] = work.tile([P, F], F32, name="h", bufs=2, align_bytes=64)
-            span = slice(fg * BANK, (fg + 1) * BANK)
-            nc.vector.tensor_tensor(
-                out=h_f32[i][:, span].rearrange("p (u m e) -> p u m e", u=2, e=2),
-                in0=h_banks[i, fg][:].rearrange("p (m u e) -> p u m e", u=2, e=2),
-                in1=bias_wide[:, span].rearrange("p (u m e) -> p u m e", u=2, e=2),
-                op=ALU.add,
-            )
+        def add_bias(i):
+            h_f32[i] = work.tile([P, F], F32, name="h", bufs=2, align_bytes=64)
+            for fg in range(FG):
+                span = slice(fg * GROUP, (fg + 1) * GROUP)
+                nc.vector.tensor_tensor(
+                    out=h_f32[i][:, span].rearrange("p (u m e) -> p u m e", u=2, e=2),
+                    in0=h_banks[i, fg][:].rearrange("p (m u e) -> p u m e", u=2, e=2),
+                    in1=bias_wide[:, span].rearrange("p (u m e) -> p u m e", u=2, e=2),
+                    op=ALU.add,
+                )
 
         def leaky(i):
-            a_bf16[i] = work.tile([P, F], BF16, name="ab", bufs=2, align_bytes=64)
+            a_bf16[i] = work.tile([P, F], BF16, name="a", bufs=2, align_bytes=64)
             nc.vector.scalar_tensor_tensor(
                 out=a_bf16[i][:], in0=h_f32[i][:], scalar=SLOPE, in1=h_f32[i][:], op0=ALU.mult, op1=ALU.max
             )
+
+
+        growth, y_f32, y_bf16, y_grouped = {}, {}, {}, {}
 
         def rates(i):
             codes, plane = a_mx[i]
             for n in range(NG):
                 if n % 2 == 0:
-                    growth[i, n // 2] = work.tile([P, HALF], F32, name="e", bufs=4, align_bytes=64)
+                    growth[i, n // 2] = work.tile([P, HALF], F32, name="growth", bufs=4, align_bytes=64)
                 bank = next_bank()
                 for fg in range(FG):
                     nc.tensor.matmul_mx(
                         out=bank[:],
                         lhsT=codes[:, fg * P : (fg + 1) * P].bitcast(FP8X4),
                         lhsT_scale=plane[:, fg * P : (fg + 1) * P],
-                        rhs=w2_codes[:, fg, n * 2 * BANK : (n + 1) * 2 * BANK].bitcast(FP4X4),
-                        rhs_scale=w2_plane[:, fg, n * BANK : (n + 1) * BANK],
+                        rhs=w2_codes[:, fg, n * 2 * GROUP : (n + 1) * 2 * GROUP].bitcast(FP4X4),
+                        rhs_scale=w2_plane[:, fg, n * GROUP : (n + 1) * GROUP],
                         start=(fg == 0),
                         stop=(fg == FG - 1),
                     )
-                nc.scalar.activation(out=growth[i, n // 2][:, (n % 2) * BANK : (n % 2 + 1) * BANK], in_=bank[:], func=ACT.Exp)
+                out = growth[i, n // 2][:, (n % 2) * GROUP : (n % 2 + 1) * GROUP]
+                nc.scalar.activation(out=out, in_=bank[:], func=ACT.Exp)
 
-        def scale_y(i, half, lo=0, hi=HALF):
-            if half == 0 and lo == 0:
+        def scale_y(i, lo, hi):
+            if lo == 0:
                 y_f32[i] = work.tile([P, N], F32, name="y", bufs=3, align_bytes=64)
-                y_bf16[i] = work.tile([P, N], BF16, name="yb", bufs=4, align_bytes=64)
+                y_bf16[i] = work.tile([P, N], BF16, name="y_rounded", bufs=4, align_bytes=64)
+            half, within = lo // HALF, slice(lo % HALF, lo % HALF + hi - lo)
             nc.vector.scalar_tensor_tensor(
-                out=y_f32[i][:, half * HALF + lo : half * HALF + hi],
-                in0=growth[i, half][:, lo:hi],
+                out=y_f32[i][:, lo:hi],
+                in0=growth[i, half][:, within],
                 scalar=thr[:, i : i + 1],
-                in1=base_wide[half][:, lo:hi],
+                in1=base_wide[half][:, within],
                 op0=ALU.mult,
                 op1=ALU.mult,
             )
 
-        def round_y(i, half, engine=None, g=None):
-            span = slice(half * HALF, (half + 1) * HALF)
-            dst = y_bf16[i][:, span].rearrange("p (u m e) -> p u m e", u=2, e=2)
-            src = y_f32[i][:, span].rearrange("p (m u e) -> p u m e", u=2, e=2)
-            if g is not None:
-                dst, src = dst[:, :, g * P : (g + 1) * P, :], src[:, :, g * P : (g + 1) * P, :]
-            copy_on(engine or CASTS[i][half], dst, src)
-
         def store_y(i, lo, hi):
             nc.sync.dma_start(out=out_0[i * P : (i + 1) * P, lo:hi], in_=y_f32[i][:, lo:hi])
 
-        def span_of(spans, i):
-            return [a <= i < b for a, b in spans].index(True)
+        def rounding_views(i, half):
+            span = slice(half * HALF, (half + 1) * HALF)
+            dst = y_bf16[i][:, span].rearrange("p (u m e) -> p u m e", u=2, e=2)
+            src = y_f32[i][:, span].rearrange("p (m u e) -> p u m e", u=2, e=2)
+            return dst, src
+
+        def round_on_gpsimd(i, half):
+            dst, src = rounding_views(i, half)
+            nc.gpsimd.tensor_scalar(out=dst, in0=src, scalar1=1.0, scalar2=0.0, op0=ALU.mult, op1=ALU.add)
+
+        def round_on_scalar(i, half):
+            dst, src = rounding_views(i, half)
+            nc.scalar.copy(out=dst, in_=src)
+
+        def round_group_on_vector(i, n):
+            dst, src = rounding_views(i, n // 2)
+            words = slice((n % 2) * P, (n % 2 + 1) * P)
+            nc.vector.tensor_copy(out=dst[:, :, words, :], in_=src[:, :, words, :])
 
         def turn_y(i, half):
-            j = span_of(quant_spans, i)
-            a, b = quant_spans[j]
-            if half == 0 and i == a:
-                y_grouped[j] = work.tile([P, NG, (b - a) * PASS], BF16, name="yg", bufs=3, align_bytes=64)
+            if half == 0:
+                y_grouped[i] = work.tile([P, N], BF16, name="y_grouped", bufs=4, align_bytes=64)
             bank = next_bank()
             words = y_bf16[i][:].bitcast(F32)
             for g in range(2):
                 for u in range(2):
-                    lo = half * BANK + (2 * u + g) * P
+                    lo = half * GROUP + (2 * u + g) * P
                     nc.tensor.transpose(bank[:, (2 * g + u) * P : (2 * g + u + 1) * P], words[:, lo : lo + P], ident_f32[:])
+            words_out = y_grouped[i][:, half * HALF : (half + 1) * HALF].bitcast(F32)
             nc.scalar.copy(
-                out=y_grouped[j][:, 2 * half : 2 * half + 2, (i - a) * PASS : (i - a + 1) * PASS].bitcast(F32).rearrange("p g (m u) -> p g m u", u=2),
+                out=words_out.rearrange("p (g m u) -> p g m u", g=2, u=2),
                 in_=bank[:].rearrange("p (g u m) -> p g m u", g=2, u=2),
             )
 
-        def window(tiles, spans, a, b, n):
-            j = span_of(spans, a)
-            return tiles[j][:, n, (a - spans[j][0]) * P : (b - spans[j][0]) * P]
+        def window(tiles, spans, i, n):
+            j = [a <= i < b for a, b in spans].index(True)
+            lo = (i - spans[j][0]) * P
+            return tiles[j][:, n, lo : lo + P]
 
-        def quant_y(j, groups):
-            a, b = quant_spans[j]
+        def quant_y(i, groups):
             for n in groups:
                 nc.vector.quantize_mx(
-                    out=window(y_codes, code_spans, a, b, n).bitcast(FP8X4),
-                    scales=window(y_plane, plane_spans, a, b, n),
-                    in_=y_grouped[j][:, n, :],
+                    out=window(y_codes, CODE_SPANS, i, n).bitcast(FP8X4),
+                    scales=window(y_plane, PLANE_SPANS, i, n),
+                    in_=y_grouped[i][:, n * GROUP : (n + 1) * GROUP],
                 )
 
         def store_codes(j, groups):
-            a, b = code_spans[j]
+            a, b = CODE_SPANS[j]
             nc.sync.dma_start(
                 out=out_1.rearrange("g p m t -> p g (m t)")[:, groups, PACK * P * a : PACK * P * b].bitcast(I32),
                 in_=y_codes[j][:, groups, :].bitcast(I32),
             )
 
         def store_scales(j, queue):
-            a, b = plane_spans[j]
+            a, b = PLANE_SPANS[j]
             for r in range(4):
                 queue.dma_start(
                     out=out_2[:, r:16:4, a * P : b * P].rearrange("g q m -> q g m").bitcast(I32),
                     in_=y_plane[j][r:P:32, :, :].bitcast(I32),
                 )
 
-        def store_planes(i):
-            for j, span in enumerate(code_spans):
+        def planes(i):
+            quant_y(i, range(NG))
+            for j, span in enumerate(CODE_SPANS):
                 if span[1] == i + 1:
                     store_codes(j, slice(0, NG))
-            if i + 1 == plane_spans[0][1]:
+            if PLANE_SPANS[0][1] == i + 1:
                 store_scales(0, nc.sync)
 
-        turn_bias()
         turn(0, None)
-        spread_bias()
         quant(0, None)
-        turn(1, None)
-        copy_bias()
-        quant(1, None)
+        spread_bias()
         hidden(0)
+        turn(1, None)
         turn(2, None)
-        turn_rows_pe()
+        add_bias(0)
+        quant(1, None)
+        turn_rows()
         hidden(1)
-        add_bias(0, 0)
-        add_bias(0, 1)
-        turn_rows_copy()
         leaky(0)
         quant(2, None)
-        add_bias(1, 0)
-        add_bias(1, 1)
-        spread(base_wide[0], base_cols, 0)
+        add_bias(1)
         turn(3, 0)
+        spread(base_wide[0], base_cols, 0)
         hidden(2)
         leaky(1)
         quant(3, 0)
         turn(None, 1)
-        spread(base_wide[1], base_cols, HALF // P)
+        spread(base_wide[1], base_cols, SPREAD)
         rates(0)
-        add_bias(2, 0)
-        add_bias(2, 1)
+        add_bias(2)
         quant(None, 1)
         leaky(2)
-        last = TILES - 1
-        for s in range(last - 2):
+
+        for s in range(LAST - 2):
             if s > 0:
                 turn_y(s - 1, 0)
                 turn_y(s - 1, 1)
-            hidden(s + 3)
-            scale_y(s, 0)
-            round_y(s, 0, "G")
-            scale_y(s, 1)
-            store_y(s, 0, N)
-            round_y(s, 1, "G", 0)
-            round_y(s, 1, "S", 1)
             ahead = (s + 4 if s + 4 < TILES else None, s + 2)
             turn(*ahead)
+            hidden(s + 3)
+            scale_y(s, 0, HALF)
+            round_on_gpsimd(s, 0)
+            scale_y(s, HALF, N)
+            store_y(s, 0, N)
+            round_on_scalar(s, 1)
             rates(s + 1)
-            add_bias(s + 3, 0)
-            add_bias(s + 3, 1)
-            if s == last - 3:
-                quant(*ahead)
-                leaky(s + 3)
-            if s >= 2:
-                quant_y(s // 2 - 1, range(2 * (s % 2), 2 * (s % 2) + 2))
-                if s % 2 == 1:
-                    store_planes(s - 2)
-            if s < last - 3:
-                leaky(s + 3)
-                quant(*ahead)
-        turn(None, last)
-        turn_y(6, 0)
-        turn_y(6, 1)
-        rates(8)
-        scale_y(7, 0)
-        quant(None, last)
-        rates(last)
-        store_y(7, 0, HALF)
-        round_y(7, 0, "G")
-        scale_y(7, 1)
-        store_y(7, HALF, N)
-        quant_y(2, range(2, NG))
-        store_planes(5)
-        quant_y(3, range(NG))
-        store_planes(6)
-        round_y(7, 1, "G")
-        turn_y(7, 0)
-        turn_y(7, 1)
-        scale_y(8, 0)
-        store_y(8, 0 * HALF, 1 * HALF)
-        round_y(8, 0, "G")
-        turn_y(8, 0)
-        scale_y(8, 1)
-        store_y(8, 1 * HALF, 2 * HALF)
-        round_y(8, 1, "G")
-        turn_y(8, 1)
-        scale_y(9, 0, 0 * BANK, 1 * BANK)
-        store_y(9, 0 * BANK, 1 * BANK)
-        scale_y(9, 0, 1 * BANK, 2 * BANK)
-        store_y(9, 1 * BANK, 2 * BANK)
-        scale_y(9, 1, 0 * BANK, 1 * BANK)
-        store_y(9, 2 * BANK, 3 * BANK)
-        scale_y(9, 1, 1 * BANK, 2 * BANK)
-        store_y(9, 3 * BANK, 4 * BANK)
-        round_y(9, 0, "V", 0)
-        round_y(9, 0, "V", 1)
-        turn_y(9, 0)
-        round_y(9, 1, "V", 0)
-        round_y(9, 1, "V", 1)
-        turn_y(9, 1)
-        quant_y(4, range(NG))
-        store_planes(7)
-        quant_y(5, range(NG))
-        quant_y(6, range(2))
-        store_codes(len(code_spans) - 1, slice(0, 2))
-        quant_y(6, range(2, NG))
-        store_codes(len(code_spans) - 1, slice(2, NG))
+            add_bias(s + 3)
+            quant(*ahead)
+            leaky(s + 3)
+            if s > 0:
+                planes(s - 1)
+
+        turn(None, LAST)
+        turn_y(LAST - 3, 0)
+        turn_y(LAST - 3, 1)
+        rates(LAST - 1)
+        scale_y(LAST - 2, 0, HALF)
+        quant(None, LAST)
+        rates(LAST)
+        store_y(LAST - 2, 0, HALF)
+        round_on_gpsimd(LAST - 2, 0)
+        scale_y(LAST - 2, HALF, N)
+        store_y(LAST - 2, HALF, N)
+        planes(LAST - 3)
+        round_on_gpsimd(LAST - 2, 1)
+        turn_y(LAST - 2, 0)
+        turn_y(LAST - 2, 1)
+        for half, round_half in enumerate((round_on_scalar, round_on_gpsimd)):
+            scale_y(LAST - 1, half * HALF, (half + 1) * HALF)
+            store_y(LAST - 1, half * HALF, (half + 1) * HALF)
+            round_half(LAST - 1, half)
+            turn_y(LAST - 1, half)
+        for n in range(NG):
+            scale_y(LAST, n * GROUP, (n + 1) * GROUP)
+            store_y(LAST, n * GROUP, (n + 1) * GROUP)
+        for half in range(2):
+            round_group_on_vector(LAST, 2 * half)
+            round_group_on_vector(LAST, 2 * half + 1)
+            turn_y(LAST, half)
+        planes(LAST - 2)
+        quant_y(LAST - 1, range(NG))
+        for half in range(2):
+            quant_y(LAST, range(2 * half, 2 * half + 2))
+            store_codes(len(CODE_SPANS) - 1, slice(2 * half, 2 * half + 2))
         store_scales(1, nc.scalar)

from contextlib import ExitStack

import concourse.mybir as mybir
from concourse.masks import make_identity

M, K, F, N = 1280, 1536, 1024, 2048
SLOPE = 0.125
FLOPS = 2 * M * K * F + 2 * M * F * N

F32 = mybir.dt.float32
BF16 = mybir.dt.bfloat16
I32 = mybir.dt.int32
U32 = mybir.dt.uint32
U8 = mybir.dt.uint8
FP8X4 = mybir.dt.float8_e4m3fn_x4
FP4X4 = mybir.dt.float4_e2m1fn_x4
ACT = mybir.ActivationFunctionType
ALU = mybir.AluOpType

P = 128
PACK = 4
GROUP = P * PACK
HALF = N // 2
KG, FG, NG = K // GROUP, F // GROUP, N // GROUP
TILES = M // P
LAST = TILES - 1
ROTATING_BANKS = 6
SPREAD = HALF // P
THR_ROW = 32
CODE_SPANS = [(0, 2), (2, 4), (4, 6), (6, 7), (7, 8), (8, 10)]
PLANE_SPANS = [(0, 6), (6, 10)]


def tile_impedance_ageing_rates_h1_kernel(
    tc, spectra, w1_words, w1_scales, b1, w2_words, w2_scales, base_rate, throughput, out_0, out_1, out_2
):
    nc = tc.nc
    with ExitStack() as ctx:
        keep = ctx.enter_context(tc.tile_pool(name="keep", bufs=1))
        work = ctx.enter_context(tc.tile_pool(name="work", bufs=3))
        psum = ctx.enter_context(tc.psum_pool(name="psum", bufs=1))
        ctx.enter_context(tc.manual_schedule())

        x_raw = keep.tile([P, TILES, K], BF16, name="x_raw", align_bytes=64)
        w1_codes = keep.tile([P, FG, KG, 2 * GROUP], U8, name="w1_codes", align_bytes=64)
        w1_plane = keep.tile([P, KG, F], U8, name="w1_plane", align_bytes=64)
        w2_codes = keep.tile([P, FG, 2 * N], U8, name="w2_codes", align_bytes=64)
        w2_plane = keep.tile([P, FG, N], U8, name="w2_plane", align_bytes=64)
        y_codes = [keep.tile([P, NG, (b - a) * P], U32, name="y_codes%d" % a, align_bytes=64) for a, b in CODE_SPANS]
        y_plane = [keep.tile([P, NG, (b - a) * P], U8, name="y_plane%d" % a, align_bytes=64) for a, b in PLANE_SPANS]
        ident_f32 = keep.tile([P, P], F32, name="ident_f32", align_bytes=64)
        ident_bf16 = keep.tile([P, P], BF16, name="ident_bf16", align_bytes=64)
        bias_cols = keep.tile([P, SPREAD], BF16, name="bias_cols", align_bytes=64)
        bias_wide = keep.tile([P, F], BF16, name="bias_wide", align_bytes=64)
        rows = keep.tile([P, P], BF16, name="rows", align_bytes=64)
        base_cols = keep.tile([P, N // P], BF16, name="base_cols", align_bytes=64)
        thr = keep.tile([P, TILES], F32, name="thr", align_bytes=64)
        base_wide = [psum.tile([P, HALF], BF16, name="base_wide%d" % half) for half in range(2)]

        banks_taken = [0]

        def next_bank():
            banks_taken[0] += 1
            return psum.tile([P, GROUP], F32, name="bank%d" % (banks_taken[0] % ROTATING_BANKS))


        def load_x(i):
            nc.sync.dma_start(out=x_raw[:, i, :], in_=spectra[i * P : (i + 1) * P, :])

        def load_w1(fg):
            columns = w1_words[:, :, fg * 2 * GROUP : (fg + 1) * 2 * GROUP]
            nc.sync.dma_start(out=w1_codes[:, fg].bitcast(I32), in_=columns.rearrange("g p n -> p g n").bitcast(I32))

        def load_scales(plane, scales):
            for r in range(4):
                nc.sync.dma_start(
                    out=plane[r:P:32, :, :].bitcast(I32),
                    in_=scales[:, r:16:4, :].rearrange("g q n -> q g n").bitcast(I32),
                )

        nc.vector.memset(w1_plane[:].rearrange("p g n -> p (g n)").bitcast(U32), 0)
        nc.vector.memset(rows[:], 0.0)
        nc.vector.memset(w2_plane[:].rearrange("p g n -> p (g n)").bitcast(U32), 0)
        make_identity(nc, ident_f32[:])
        make_identity(nc, ident_bf16[:])
        load_x(0)
        nc.scalar.dma_start(out=bias_cols[:], in_=b1.rearrange("(n c) -> n c", c=SPREAD))
        load_w1(0)
        load_scales(w1_plane, w1_scales)
        load_x(1)
        load_w1(1)
        nc.gpsimd.dma_start(out=rows[0 : N // P, :], in_=base_rate.rearrange("(r c) -> r c", c=P))
        nc.gpsimd.dma_start(out=rows[THR_ROW : THR_ROW + TILES, :], in_=throughput.rearrange("(r c) -> r c", c=P))
        load_x(2)
        load_x(3)
        load_scales(w2_plane, w2_scales)
        nc.sync.dma_start(out=w2_codes[:].bitcast(I32), in_=w2_words.rearrange("g p n -> p g n").bitcast(I32))
        for i in range(4, TILES):
            load_x(i)


        def spread(wide, cols, first):
            for c in range(SPREAD):
                column = cols[:, first + c : first + c + 1].to_broadcast([P, P])
                nc.tensor.transpose(wide[:, c * P : (c + 1) * P], column, ident_bf16[:])

        def spread_bias():
            wide = next_bank()[:].bitcast(BF16)
            spread(wide, bias_cols, 0)
            src = wide.rearrange("p (b u e g a) -> p g u a b e", b=2, u=2, e=2, g=FG)
            dst = bias_wide[:].rearrange("p (g u a b e) -> p g u a b e", b=2, u=2, e=2, g=FG)
            for fg in range(FG):
                for u in range(2):
                    nc.vector.tensor_copy(out=dst[:, fg, u], in_=src[:, fg, u])

        def turn_rows():
            columns = next_bank()[:].bitcast(BF16)[:, 0:P]
            nc.tensor.transpose(columns, rows[:], ident_bf16[:])
            nc.vector.tensor_copy(out=base_cols[:], in_=columns[:, 0 : N // P])
            nc.scalar.activation(out=thr[:], in_=columns[:, THR_ROW : THR_ROW + TILES], func=ACT.Identity)


        grouped, x_mx, h_banks, h_f32, a_bf16, a_mx = {}, {}, {}, {}, {}, {}

        def turn(xi, ai):
            pairs = []
            if xi is not None:
                words = x_raw[:, xi, :].bitcast(F32)
                pairs += [[words[:, 2 * P * g + u : 2 * P * (g + 1) : 2] for u in range(2)] for g in range(KG)]
            if ai is not None:
                words = a_bf16[ai][:].bitcast(F32)
                pairs += [[words[:, (2 * g + u) * P : (2 * g + u + 1) * P] for u in range(2)] for g in range(FG)]
            staged = work.tile([P, K + F], BF16, name="staged", bufs=3, align_bytes=64)
            for first in range(0, len(pairs), 2):
                bank = next_bank()
                in_bank = pairs[first : first + 2]
                count = len(in_bank)
                for g in range(count):
                    for u in range(2):
                        nc.tensor.transpose(bank[:, (2 * g + u) * P : (2 * g + u + 1) * P], in_bank[g][u], ident_f32[:])
                words_out = staged[:, first * GROUP : (first + count) * GROUP].bitcast(F32)
                nc.scalar.copy(
                    out=words_out.rearrange("p (g m u) -> p g m u", g=count, u=2),
                    in_=bank[:, 0 : count * 2 * P].rearrange("p (g u m) -> p g m u", g=count, u=2),
                )
            grouped[xi, ai] = (staged, len(pairs))

        def quant(xi, ai):
            staged, count = grouped[xi, ai]
            codes = work.tile([P, (KG + FG) * P], U32, name="codes", bufs=4, align_bytes=64)
            plane = work.tile([P, (KG + FG) * P], U8, name="plane", bufs=4, align_bytes=64)
            wide = 4 if count >= 4 else 2
            for first, stop in ((0, wide), (wide, count)):
                if stop > first:
                    nc.vector.quantize_mx(
                        out=codes[:, first * P : stop * P].bitcast(FP8X4),
                        scales=plane[:, first * P : stop * P],
                        in_=staged[:, first * GROUP : stop * GROUP],
                    )
            if xi is not None:
                x_mx[xi] = (codes[:, 0 : KG * P], plane[:, 0 : KG * P])
            if ai is not None:
                a_mx[ai] = (codes[:, (count - FG) * P : count * P], plane[:, (count - FG) * P : count * P])

        def hidden(i):
            codes, plane = x_mx[i]
            for fg in range(FG):
                bank = next_bank()
                for g in range(KG):
                    nc.tensor.matmul_mx(
                        out=bank[:],
                        lhsT=codes[:, g * P : (g + 1) * P].bitcast(FP8X4),
                        lhsT_scale=plane[:, g * P : (g + 1) * P],
                        rhs=w1_codes[:, fg, g, :].bitcast(FP4X4),
                        rhs_scale=w1_plane[:, g, fg * GROUP : (fg + 1) * GROUP],
                        start=(g == 0),
                        stop=(g == KG - 1),
                    )
                h_banks[i, fg] = bank

        def add_bias(i):
            h_f32[i] = work.tile([P, F], F32, name="h", bufs=2, align_bytes=64)
            for fg in range(FG):
                span = slice(fg * GROUP, (fg + 1) * GROUP)
                nc.vector.tensor_tensor(
                    out=h_f32[i][:, span].rearrange("p (u m e) -> p u m e", u=2, e=2),
                    in0=h_banks[i, fg][:].rearrange("p (m u e) -> p u m e", u=2, e=2),
                    in1=bias_wide[:, span].rearrange("p (u m e) -> p u m e", u=2, e=2),
                    op=ALU.add,
                )

        def leaky(i):
            a_bf16[i] = work.tile([P, F], BF16, name="a", bufs=2, align_bytes=64)
            nc.vector.scalar_tensor_tensor(
                out=a_bf16[i][:], in0=h_f32[i][:], scalar=SLOPE, in1=h_f32[i][:], op0=ALU.mult, op1=ALU.max
            )


        growth, y_f32, y_bf16, y_grouped = {}, {}, {}, {}

        def rates(i):
            codes, plane = a_mx[i]
            for n in range(NG):
                if n % 2 == 0:
                    growth[i, n // 2] = work.tile([P, HALF], F32, name="growth", bufs=4, align_bytes=64)
                bank = next_bank()
                for fg in range(FG):
                    nc.tensor.matmul_mx(
                        out=bank[:],
                        lhsT=codes[:, fg * P : (fg + 1) * P].bitcast(FP8X4),
                        lhsT_scale=plane[:, fg * P : (fg + 1) * P],
                        rhs=w2_codes[:, fg, n * 2 * GROUP : (n + 1) * 2 * GROUP].bitcast(FP4X4),
                        rhs_scale=w2_plane[:, fg, n * GROUP : (n + 1) * GROUP],
                        start=(fg == 0),
                        stop=(fg == FG - 1),
                    )
                out = growth[i, n // 2][:, (n % 2) * GROUP : (n % 2 + 1) * GROUP]
                nc.scalar.activation(out=out, in_=bank[:], func=ACT.Exp)

        def scale_y(i, lo, hi):
            if lo == 0:
                y_f32[i] = work.tile([P, N], F32, name="y", bufs=3, align_bytes=64)
                y_bf16[i] = work.tile([P, N], BF16, name="y_rounded", bufs=4, align_bytes=64)
            half, within = lo // HALF, slice(lo % HALF, lo % HALF + hi - lo)
            nc.vector.scalar_tensor_tensor(
                out=y_f32[i][:, lo:hi],
                in0=growth[i, half][:, within],
                scalar=thr[:, i : i + 1],
                in1=base_wide[half][:, within],
                op0=ALU.mult,
                op1=ALU.mult,
            )

        def store_y(i, lo, hi):
            nc.sync.dma_start(out=out_0[i * P : (i + 1) * P, lo:hi], in_=y_f32[i][:, lo:hi])

        def rounding_views(i, half):
            span = slice(half * HALF, (half + 1) * HALF)
            dst = y_bf16[i][:, span].rearrange("p (u m e) -> p u m e", u=2, e=2)
            src = y_f32[i][:, span].rearrange("p (m u e) -> p u m e", u=2, e=2)
            return dst, src

        def round_on_gpsimd(i, half):
            dst, src = rounding_views(i, half)
            nc.gpsimd.tensor_scalar(out=dst, in0=src, scalar1=1.0, scalar2=0.0, op0=ALU.mult, op1=ALU.add)

        def round_on_scalar(i, half):
            dst, src = rounding_views(i, half)
            nc.scalar.copy(out=dst, in_=src)

        def round_group_on_vector(i, n):
            dst, src = rounding_views(i, n // 2)
            words = slice((n % 2) * P, (n % 2 + 1) * P)
            nc.vector.tensor_copy(out=dst[:, :, words, :], in_=src[:, :, words, :])

        def turn_y(i, half):
            if half == 0:
                y_grouped[i] = work.tile([P, N], BF16, name="y_grouped", bufs=4, align_bytes=64)
            bank = next_bank()
            words = y_bf16[i][:].bitcast(F32)
            for g in range(2):
                for u in range(2):
                    lo = half * GROUP + (2 * u + g) * P
                    nc.tensor.transpose(bank[:, (2 * g + u) * P : (2 * g + u + 1) * P], words[:, lo : lo + P], ident_f32[:])
            words_out = y_grouped[i][:, half * HALF : (half + 1) * HALF].bitcast(F32)
            nc.scalar.copy(
                out=words_out.rearrange("p (g m u) -> p g m u", g=2, u=2),
                in_=bank[:].rearrange("p (g u m) -> p g m u", g=2, u=2),
            )

        def window(tiles, spans, i, n):
            j = [a <= i < b for a, b in spans].index(True)
            lo = (i - spans[j][0]) * P
            return tiles[j][:, n, lo : lo + P]

        def quant_y(i, groups):
            for n in groups:
                nc.vector.quantize_mx(
                    out=window(y_codes, CODE_SPANS, i, n).bitcast(FP8X4),
                    scales=window(y_plane, PLANE_SPANS, i, n),
                    in_=y_grouped[i][:, n * GROUP : (n + 1) * GROUP],
                )

        def store_codes(j, groups):
            a, b = CODE_SPANS[j]
            nc.sync.dma_start(
                out=out_1.rearrange("g p m t -> p g (m t)")[:, groups, PACK * P * a : PACK * P * b].bitcast(I32),
                in_=y_codes[j][:, groups, :].bitcast(I32),
            )

        def store_scales(j, queue):
            a, b = PLANE_SPANS[j]
            for r in range(4):
                queue.dma_start(
                    out=out_2[:, r:16:4, a * P : b * P].rearrange("g q m -> q g m").bitcast(I32),
                    in_=y_plane[j][r:P:32, :, :].bitcast(I32),
                )

        def planes(i):
            quant_y(i, range(NG))
            for j, span in enumerate(CODE_SPANS):
                if span[1] == i + 1:
                    store_codes(j, slice(0, NG))
            if PLANE_SPANS[0][1] == i + 1:
                store_scales(0, nc.sync)

        turn(0, None)
        quant(0, None)
        spread_bias()
        hidden(0)
        turn(1, None)
        turn(2, None)
        add_bias(0)
        quant(1, None)
        turn_rows()
        hidden(1)
        leaky(0)
        quant(2, None)
        add_bias(1)
        turn(3, 0)
        spread(base_wide[0], base_cols, 0)
        hidden(2)
        leaky(1)
        quant(3, 0)
        turn(None, 1)
        spread(base_wide[1], base_cols, SPREAD)
        rates(0)
        add_bias(2)
        quant(None, 1)
        leaky(2)

        for s in range(LAST - 2):
            if s > 0:
                turn_y(s - 1, 0)
                turn_y(s - 1, 1)
            ahead = (s + 4 if s + 4 < TILES else None, s + 2)
            turn(*ahead)
            hidden(s + 3)
            scale_y(s, 0, HALF)
            round_on_gpsimd(s, 0)
            scale_y(s, HALF, N)
            store_y(s, 0, N)
            round_on_scalar(s, 1)
            rates(s + 1)
            add_bias(s + 3)
            quant(*ahead)
            leaky(s + 3)
            if s > 0:
                planes(s - 1)

        turn(None, LAST)
        turn_y(LAST - 3, 0)
        turn_y(LAST - 3, 1)
        rates(LAST - 1)
        scale_y(LAST - 2, 0, HALF)
        quant(None, LAST)
        rates(LAST)
        store_y(LAST - 2, 0, HALF)
        round_on_gpsimd(LAST - 2, 0)
        scale_y(LAST - 2, HALF, N)
        store_y(LAST - 2, HALF, N)
        planes(LAST - 3)
        round_on_gpsimd(LAST - 2, 1)
        turn_y(LAST - 2, 0)
        turn_y(LAST - 2, 1)
        for half, round_half in enumerate((round_on_scalar, round_on_gpsimd)):
            scale_y(LAST - 1, half * HALF, (half + 1) * HALF)
            store_y(LAST - 1, half * HALF, (half + 1) * HALF)
            round_half(LAST - 1, half)
            turn_y(LAST - 1, half)
        for n in range(NG):
            scale_y(LAST, n * GROUP, (n + 1) * GROUP)
            store_y(LAST, n * GROUP, (n + 1) * GROUP)
        for half in range(2):
            round_group_on_vector(LAST, 2 * half)
            round_group_on_vector(LAST, 2 * half + 1)
            turn_y(LAST, half)
        planes(LAST - 2)
        quant_y(LAST - 1, range(NG))
        for half in range(2):
            quant_y(LAST, range(2 * half, 2 * half + 2))
            store_codes(len(CODE_SPANS) - 1, slice(2 * half, 2 * half + 2))
        store_scales(1, nc.scalar)
